import numpy as np, ml_dtypes
CORES = [33,161,289,417,57,185,313,441]
N = 8
R, L = 4096, 1024
CAPP = 256
def entries(a): return a.T.reshape(-1)
def pack(v, P): return np.ascontiguousarray(np.asarray(v, np.int32).reshape(-1, P).T)
def lists(rng, how):
    n = N * L
    P = rng.permutation(np.repeat(np.arange(N * N), CAPP))[:n]
    if how == "full":
        a, b = rng.permutation(N)[:2]; o = rng.permutation(N * N); o = o[(o // N != a) & (o % N != b)]
        C = np.concatenate([N * a + rng.permutation(np.delete(np.arange(N), b)), [N * a + b], N * rng.permutation(np.delete(np.arange(N), a)) + b, o])[:n // CAPP]
        P = np.repeat(C, CAPP).reshape(N, L)[rng.permutation(N)].reshape(-1)
    h, g = P // N, P % N
    d = np.zeros(n, np.int64)
    for q in range(N): m = np.nonzero(g == q)[0]; d[m] = R * q + np.concatenate([[0, R - 1], 1 + rng.permutation(R - 2)])[:len(m)]
    s = R * h + rng.integers(0, R, n)
    if how == "fork": s = R * h + rng.integers(0, R, N)[h]
    if how == "chain":
        for q in range(N):
            m = np.nonzero(h == q)[0]; w = d[g == q]
            if len(w): s[m] = w[rng.integers(0, len(w), len(m))]
    if how == "gaps":
        z = rng.permutation(N)[:3]; k = (rng.random(n) < 0.5) | (np.arange(n) // L == z[0]) | (h == z[1]) | (g == z[2]); s[k] = -1; d[k] = -1
    return {"src": np.stack([pack(v, 16) for v in s.reshape(N, L)]), "dst": np.stack([pack(v, 16) for v in d.reshape(N, L)])}
def setup_inputs(rng):
    return dict({"tab": rng.standard_normal((N, 128, R), dtype=np.float32).astype(ml_dtypes.bfloat16)}, **lists(rng, "uniform"))
def setup_inputs_chain(rng):
    d = setup_inputs(rng); d.update(lists(rng, "chain"))
    for k in ("tab",): d[k] = (d[k].astype(np.float32) * 1048576.0).astype(d[k].dtype)
    return d
def setup_inputs_fork(rng):
    d = setup_inputs(rng); d.update(lists(rng, "fork"))
    for k in ("tab",): d[k] = (d[k].astype(np.float32) * (1 / 1024.0)).astype(d[k].dtype)
    return d
def setup_inputs_full(rng):
    d = setup_inputs(rng); d.update(lists(rng, "full"))
    return d
def setup_inputs_gaps(rng):
    d = setup_inputs(rng); d.update(lists(rng, "gaps"))
    return d
def check_inputs(x):
    bad = []; s, d = x["src"].reshape(-1), x["dst"].reshape(-1); k = d >= 0
    if s.min() < -1 or s.max() >= N * R or d.min() < -1 or d.max() >= N * R: bad.append("out of range")
    if ((s < 0) != (d < 0)).any(): bad.append("half a pair")
    if len(np.unique(d[k])) != int(k.sum()): bad.append("a column is written twice")
    if k.any() and int(np.bincount(s[k] // R * N + d[k] // R).max()) > CAPP: bad.append("more than CAPP pairs from one rank's part to one rank's part")
    return bad
def reference(tab, src, dst):
    A = np.concatenate(list(tab), axis=1); Y = A.copy()
    for r in range(N):
        s, d = entries(src[r]), entries(dst[r]); k = d >= 0
        Y[:, d[k]] = A[:, s[k]]
    return {"y": np.stack([Y[:, R * r:R * r + R] for r in range(N)])}

@@ -1,0 +1,376 @@
+from concourse.bass import DstId, RemoteDMATransfer
+from concourse.mybir import dt, AluOpType as A, ActivationFunctionType as F
+
+N, R, CAP = 8, 4096, 256
+MW = CAP + 32
+PAD = 384
+SLOT0 = 1153
+WIN = SLOT0 + N * CAP
+LW = 96
+
+SCRATCH = {
+    "ki": ("sbuf", [128, 1], "int32"),
+    "xi": ("sbuf", [128, 256], "int32"),
+    "ti": ("sbuf", [128, 16], "int32"),
+    "tr": ("sbuf", [128, 64], "float32"),
+    "kb": ("sbuf", [128, 4], "int32"),
+    "kf": ("sbuf", [128, 8], "float32"),
+    "kc": ("sbuf", [128, 8], "float32"),
+    "x15": ("sbuf", [128, 128], "int32"),
+    "xs4": ("sbuf", [128, 128], "int32"),
+    "xs3": ("sbuf", [128, 32], "int32"),
+    "th": ("sbuf", [128, 32], "int32"),
+    "rep": ("sbuf", [128, 128], "bfloat16"),
+    "eye": ("sbuf", [128, 128], "bfloat16"),
+    "za": ("sbuf", [128, 240], "bfloat16"),
+    "zc": ("sbuf", [128, 240], "bfloat16"),
+    "la": ("sbuf", [128, 128], "float32"),
+    "lb": ("sbuf", [128, 128], "float32"),
+    "ltri": ("sbuf", [128, 128], "float32"),
+    "gx": ("sbuf", [128, 144], "bfloat16"),
+    "wr": ("sbuf", [128, 32], "bfloat16"),
+    "dtr": ("sbuf", [128, 32], "bfloat16"),
+    "ld": ("sbuf", [128, 128], "int32"),
+    "dg": ("sbuf", [128, 384], "int32"),
+    "xb": ("sbuf", [128, 320], "bfloat16"),
+    "lists": ("sbuf", [128, N, LW], "bfloat16"),
+    "mm": ("sbuf", [128, 512], "bfloat16"),
+    "mb": ("sbuf", [128, 512], "bfloat16"),
+    "me": ("sbuf", [128, 512], "bfloat16"),
+    "junk": ("sbuf", [128, 512], "bfloat16"),
+    "tot": ("sbuf", [128, 1], "float32"),
+    "lin": ("sbuf", [128, 1024], "bfloat16"),
+    "offf": ("sbuf", [128, 64], "float32"),
+    "offs": ("sbuf", [128, 64], "uint16"),
+    "win": ("sbuf", [128, WIN + 7], "bfloat16"),
+    "xsb": ("sbuf", [128, 512], "bfloat16"),
+    "g16": ("sbuf", [128, 128], "uint16"),
+    "tabw": ("sbuf", [128, PAD + R], "bfloat16"),
+    "msg": ("sbuf", [128, N, MW], "bfloat16"),
+    "land": ("sbuf", [128, N, MW], "bfloat16"),
+    "dsum": ("sbuf", [128, 128], "int32"),
+    "dof": ("sbuf", [128, 128], "uint16"),
+    "psl": ("psum", [128, 512], "float32"),
+    "pss": ("psum", [128, 512], "float32"),
+    "psb": ("psum", [128, 512], "float32"),
+    "pso": ("psum", [128, 512], "float32"),
+    "psn": ("psum", [128, 1024], "float32"),
+    "psx": ("psum", [128, 512], "float32"),
+    "psg": ("psum", [128, 512], "float32"),
+}
+_EV = ["io1", "io2", "c1", "c2", "c3", "lds", "ldd", "lo", "lx", "lp", "lready", "k1", "k2", "k3", "tabl",
+       "mrow", "scn", "tt", "bas", "ee", "em", "po", "mx", "of", "lnp", "lnc", "wz", "sc", "x1", "xc1", "xc2",
+       "pg", "gc", "pd", "ysy", "ysc"]
+SEMAPHORES = (_EV + ["gp%d" % k for k in range(4)] + ["da%d" % k for k in range(N)] + ["db%d" % k for k in range(N)]
+              + ["dc%d" % k for k in range(N)] + ["de%d" % k for k in range(N)]
+              + ["lar0", "lar1", "lsent", "dsent", "fsent"])
+
+
+def _chip_cores(core, topo):
+    return [c for c in range(128 * topo.host(core), 128 * topo.host(core) + 128) if topo.chip(c) == topo.chip(core)]
+
+
+def _routes(T, topo):
+    cores = T.cores
+    kind, relay, used = {}, {}, set(cores)
+
+    def take(near, dst, other_die):
+        cand = [c for c in _chip_cores(near, topo) if c not in used and topo.may_write(c, dst)]
+        cand.sort(key=lambda c: (sum(1 for d in cores if topo.may_write(c, d)), (topo.die(c) == topo.die(near)) == other_die, c))
+        used.add(cand[0])
+        return cand[0]
+
+    n = len(cores)
+    for a in range(n):
+        for b in range(n):
+            if a == b:
+                continue
+            ca, cb = cores[a], cores[b]
+            if topo.may_write(ca, cb):
+                kind[(a, b)] = "Dr" if topo.same_plane(ca, cb) else "Dc"
+                relay[(a, b)] = None
+    reach = lambda a, b: any(topo.may_write(c, cores[b]) for c in _chip_cores(cores[a], topo))
+    for a in range(n):
+        nb = {kind[(a, x)]: x for x in range(n) if (a, x) in kind and kind[(a, x)] in ("Dr", "Dc")}
+        for b in range(n):
+            if a != b and not reach(a, b):
+                same = topo.chip(cores[a]) == topo.chip(cores[b])
+                kind[(a, b)] = "Fe" if same else "Fo"
+                relay[(a, b)] = take(cores[nb["Dr" if same else "Dc"]], cores[b], same)
+    for a in range(n):
+        for b in range(n):
+            if a != b and (a, b) not in kind:
+                ca, cb = cores[a], cores[b]
+                if topo.host(ca) == topo.host(cb):
+                    kind[(a, b)] = "O0"
+                elif topo.rack(topo.host(ca)) == topo.rack(topo.host(cb)):
+                    kind[(a, b)] = "O1"
+                else:
+                    kind[(a, b)] = "O2"
+                relay[(a, b)] = take(ca, cb, True)
+    return kind, relay
+
+
+_CACHE = {}
+
+
+def _bits(m):
+    return [i for i in range(16) if (m >> i) & 1]
+
+
+def rank_program(g, core, T, topo):
+    if "r" not in _CACHE:
+        _CACHE["r"] = _routes(T, topo)
+    kind, relay = _CACHE["r"]
+    S = T.sem
+    rank = T.rank_of(core)
+    if rank is None:
+        for (a, b), c in relay.items():
+            if c == core:
+                _relay(g, core, T, topo, a, b)
+        return
+    _rank(g, core, rank, T, topo, kind, relay)
+
+
+def _relay(g, core, T, topo, a, b):
+    S = T.sem
+    dst = T.cores[b]
+    rid, pid = topo.addr(dst, core)
+    m = topo.mask(core, dst)
+    nm = len(_bits(m))
+    g.wait_ge(S["lar0"], 8)
+    g.remote_dma(T.lists[:, a, :], T.lists[:, a, :], S["lar1"], S["fsent"], pid, rid, m)
+    g.wait_ge(S["da%d" % a], 4)
+    g.remote_dma(T.land[:, a, :], T.land[:, a, :], S["da%d" % a], S["fsent"], pid, rid, m)
+    g.wait_ge(S["fsent"], 2 * nm)
+
+
+def _rank(g, core, a, T, topo, kind, relay):
+    S = T.sem
+    V, P, C, Y = g.vector, g.tensor, g.scalar, g.sync
+    cnt = {}
+
+    def ev(ins, name, n=1):
+        ins.then_inc(S[name], n)
+        cnt[name] = cnt.get(name, 0) + n
+
+    def w(q, name):
+        q.wait_ge(S[name], cnt[name])
+
+    by = {kind[(a, b)]: b for b in range(N) if b != a}
+    frm = {kind[(s, a)]: s for s in range(N) if s != a}
+    first = {b: (T.cores[b] if relay[(a, b)] is None else relay[(a, b)]) for b in range(N) if b != a}
+    order = ["Fe", "Fo", "O1", "O2", "O0", "Dc", "Dr"]
+    off_mask = topo.mask(core, first[by["Dr"]])
+    eng = _bits(off_mask)
+    half = [sum(1 << e for e in eng[:4]), sum(1 << e for e in eng[4:])]
+
+    ev(Y.dma_start(T.ld[0:16, 0:64], T.src[:, :]), "lds", 16)
+    ev(C.dma_start(T.ld[0:16, 64:128], T.dst[:, :]), "ldd", 16)
+    ev(g.iota(T.ki[:, :], [[1, 1]], 0, 1), "io1")
+    ev(g.iota(T.xi[:, :], [[1, 256]], 0, 0), "io1")
+    ev(g.iota(T.ti[:, :], [[16, 16]], 0, 1), "io2")
+    ev(g.iota(T.tr[:, :], [[16, 64]], 0, 1, allow_small_or_imprecise_dtypes=True), "io2")
+
+    def ts(out, in0, s1, s2, op0, op1=None):
+        if op1 is None:
+            return V.tensor_scalar(out=out, in0=in0, scalar1=s1, scalar2=None, op0=op0)
+        return V.tensor_scalar(out=out, in0=in0, scalar1=s1, scalar2=s2, op0=op0, op1=op1)
+
+    w(V, "io1")
+    ev(ts(T.kb[:, 0:1], T.ki[:, :], 15, None, A.bitwise_and), "c1")
+    ev(ts(T.kb[:, 1:2], T.ki[:, :], 4, None, A.arith_shift_right), "c1")
+    ev(ts(T.kb[:, 2:3], T.ki[:, :], 31, None, A.bitwise_and), "c1")
+    ev(ts(T.kb[:, 3:4], T.ki[:, :], 5, None, A.arith_shift_right), "c1")
+    ev(ts(T.x15[:, :], T.xi[:, 0:128], 15, None, A.bitwise_and), "c1")
+    w(V, "c1")
+    ev(V.tensor_copy(out=T.kf[:, 0:4], in_=T.kb[:, :]), "c2")
+    ev(V.tensor_copy(out=T.kf[:, 4:5], in_=T.ki[:, :]), "c2")
+    w(V, "c2")
+    ev(ts(T.rep[0:16, :], T.x15[0:16, :], T.kf[0:16, 4:5], None, A.is_equal), "c3")
+    ev(ts(T.eye[:, :], T.xi[:, 0:128], T.kf[:, 4:5], None, A.is_equal), "c3")
+
+    w(V, "lds")
+    w(V, "ldd")
+    src, dst = T.ld[0:16, 0:64], T.ld[0:16, 64:128]
+    d = lambda k: T.dg[0:16, 64 * k:64 * k + 64]
+    ev(ts(d(0), src, 0xF000, None, A.bitwise_and), "lo")
+    ev(ts(d(1), dst, 3, 0x1E00, A.arith_shift_right, A.bitwise_and), "lo")
+    ev(ts(d(2), src, 4032, None, A.bitwise_and), "lo")
+    ev(ts(d(3), src, 63, None, A.bitwise_and), "lo")
+    ev(ts(d(4), dst, 4064, None, A.bitwise_and), "lo")
+    ev(ts(d(5), dst, 31, None, A.bitwise_and), "lo")
+    w(V, "lo")
+    ev(V.tensor_tensor(out=T.xb[0:16, 0:64], in0=d(0), in1=d(1), op=A.add), "lx")
+    ev(V.tensor_copy(out=T.xb[0:16, 64:192], in_=T.dg[0:16, 128:256]), "lx")
+    ev(ts(T.xb[0:16, 192:256], d(4), float(PAD - 32), None, A.add), "lx")
+    ev(ts(T.xb[0:16, 256:320], d(5), 32.0, None, A.add), "lx")
+    w(P, "c3")
+    w(P, "lx")
+    ev(P.matmul(T.psl[:, 0:64], T.rep[0:16, :], T.xb[0:16, 0:64], True, True), "lp")
+    ev(P.matmul(T.psl[:, 64:80], T.xb[0:16, 64:320:2], T.eye[0:16, 0:16], True, True), "lp")
+    ev(P.matmul(T.psl[:, 80:96], T.xb[0:16, 65:320:2], T.eye[0:16, 0:16], True, True), "lp")
+    w(V, "lp")
+    ev(V.tensor_copy(out=T.lists[:, a, :], in_=T.psl[:, 0:96]), "lready")
+
+    w(g, "lready")
+    ids, outs = [], []
+    for k in order:
+        rid, pid = topo.addr(first[by[k]], core)
+        ids.append(DstId(rid=rid, pnc=pid))
+        outs.append(T.lists[:, a, :])
+    g.remote_dma_fused([RemoteDMATransfer(dst_ids=ids, dma_engine_mask=off_mask, remote_sem=S["lar0"],
+                                          srcs=[T.lists[:, a, :]], dsts=outs)], local_sem=S["lsent"])
+    Y.wait_ge(S["lsent"], len(eng))
+    ev(Y.dma_start(T.tabw[:, PAD:PAD + R], T.tab[:, :]), "tabl", 16)
+
+    w(V, "c3")
+    w(V, "io2")
+    kf, kc = T.kf, T.kc
+    ev(ts(kc[:, 0:1], kf[:, 1:2], 512.0, 4096.0 * a, A.mult, A.add), "k1")
+    ev(ts(kc[:, 1:2], kf[:, 1:2], 256.0, float(SLOT0 - 1), A.mult, A.add), "k1")
+    ev(ts(kc[:, 2:3], kf[:, 2:3], 4.0, None, A.mult), "k1")
+    ev(ts(T.xs4[:, :], T.xi[:, 0:128], 4, None, A.arith_shift_right), "k1")
+    ev(ts(T.xs3[:, :], T.xi[:, 0:32], 3, None, A.arith_shift_right), "k1")
+    ev(ts(T.th[:, 0:16], T.ti[:, :], 0x7FE0, None, A.bitwise_and), "k1")
+    ev(ts(T.th[:, 16:32], T.ti[:, :], 31, None, A.bitwise_and), "k1")
+    ev(V.memset(T.za[:, :], 0.0), "k1")
+    ev(V.memset(T.zc[:, :], 0.0), "k1")
+    ev(ts(T.lb[:, :], T.xi[:, 0:128], kf[:, 4:5], None, A.is_gt), "k1")
+    w(V, "k1")
+    ev(V.tensor_tensor(out=kc[:, 3:4], in0=kc[:, 2:3], in1=kf[:, 3:4], op=A.add), "k2")
+    ev(ts(T.la[:, :], T.xs4[:, :], kf[:, 1:2], None, A.is_equal), "k2")
+    w(V, "k2")
+    ev(V.tensor_tensor(out=T.ltri[:, :], in0=T.la[:, :], in1=T.lb[:, :], op=A.mult), "k3")
+    ev(ts(T.gx[:, :], T.xi[:, 0:144], kc[:, 3:4], None, A.is_equal), "k3")
+    ev(ts(T.wr[:, :], T.xs3[:, :], kf[:, 0:1], None, A.is_equal), "k3")
+    ev(ts(T.za[:, 112:128], T.xi[:, 0:16], kf[:, 0:1], None, A.is_equal), "k3")
+    ev(ts(T.zc[:, 112:128], T.xi[:, 0:16], kf[:, 0:1], kc[:, 1:2], A.is_equal, A.mult), "k3")
+    ev(V.tensor_copy(out=T.dtr[:, 0:32:2], in_=T.th[:, 0:16]), "k3")
+    ev(V.tensor_copy(out=T.dtr[:, 1:32:2], in_=T.th[:, 16:32]), "k3")
+    ev(V.memset(T.win[:, SLOT0:WIN], 0.0), "k3")
+    w(V, "k3")
+
+    def mrow(r):
+        ev(ts(T.mm[:, r:512:8], T.lists[:, r, 0:64], kc[:, 0:1], None, A.is_equal), "mrow")
+
+    mrow(a)
+    V.wait_ge(S["lar0"], 16)
+    mrow(frm["Dr"])
+    mrow(frm["Dc"])
+    V.wait_ge(S["lar1"], 40)
+    for k in ("Fe", "Fo", "O0", "O1", "O2"):
+        mrow(frm[k])
+    w(V, "mrow")
+    ev(V.tensor_tensor_scan(out=T.pss[:, :], data0=T.mm[:, :], data1=T.mm[:, :], initial=0.0, op0=A.add, op1=A.max), "scn")
+    w(P, "k3")
+    w(P, "lready")
+    P.wait_ge(S["lar0"], 16)
+    P.wait_ge(S["lar1"], 40)
+    for s in range(4):
+        for e in range(2):
+            j = 2 * s + e
+            ev(P.matmul(T.psn[:, 128 * j:128 * j + 128], T.gx[:, 4 * s:4 * s + 128], T.lists[:, :, 64 + 16 * e:80 + 16 * e], True, True), "lnp")
+    w(C, "mrow")
+    ev(C.activation(T.junk[:, :], T.mm[:, :], F.Copy, accum_out=T.tot[:, :]), "tt")
+    w(P, "tt")
+    ev(P.matmul(T.psb[:, 0:1], T.ltri[:, :], T.tot[:, :], True, True), "bas")
+    w(C, "lnp")
+    ev(C.activation(T.lin[:, 0:512], T.psn[:, 0:512], F.Copy), "lnc")
+    ev(C.activation(T.lin[:, 512:1024], T.psn[:, 512:1024], F.Copy), "lnc")
+    w(P, "mrow")
+    for q in range(8):
+        P.matmul(T.pso[:, 0:64], T.zc[:, 112 - 16 * q:240 - 16 * q], T.mm[:, 64 * q:64 * q + 64], q == 0, False)
+    w(V, "scn")
+    ev(V.tensor_tensor(out=T.me[:, :], in0=T.pss[:, :], in1=T.mm[:, :], op=A.mult), "ee")
+    w(V, "bas")
+    ev(ts(T.mb[:, :], T.mm[:, :], T.psb[:, 0:1], None, A.mult), "em")
+    w(P, "ee")
+    for q in range(8):
+        P.matmul(T.pso[:, 0:64], T.za[:, 112 - 16 * q:240 - 16 * q], T.me[:, 64 * q:64 * q + 64], False, False)
+    w(P, "em")
+    for q in range(8):
+        i = P.matmul(T.pso[:, 0:64], T.za[:, 112 - 16 * q:240 - 16 * q], T.mb[:, 64 * q:64 * q + 64], False, q == 7)
+    ev(i, "po")
+    w(V, "po")
+    ev(V.tensor_tensor(out=T.offf[:, :], in0=T.pso[:, 0:64], in1=T.tr[:, :], op=A.max), "mx")
+    w(V, "mx")
+    ev(V.tensor_copy(out=T.offs[:, :], in_=T.offf[:, :]), "of")
+    w(V, "of")
+    w(V, "lnc")
+    ev(V.tensor_copy(out=T.win[:, 0:WIN].indirect(T.offs[:, 0:64]), in_=T.lin[:, :]), "sc")
+    w(P, "sc")
+    for i in range(16):
+        ev(P.matmul(T.psx[:, i:512:16], T.win[:, SLOT0 + i:SLOT0 + i + 2033:16], T.wr[:, :], True, True), "x1")
+    w(V, "x1")
+    ev(V.tensor_copy(out=T.xsb[:, 0:256], in_=T.psx[:, 0:256]), "xc1")
+    w(P, "xc1")
+    P.matmul(T.psg[:, 0:128], T.xsb[:, 0:128], T.eye[:, :], True, False)
+    ev(P.matmul(T.psg[:, 0:128], T.xsb[:, 128:256], T.eye[:, :], False, True), "pg")
+    w(C, "xc1")
+    ev(C.activation(T.xsb[:, 256:512], T.psx[:, 256:512], F.Copy), "xc2")
+    w(V, "pg")
+    ev(V.tensor_copy(out=T.g16[:, :], in_=T.psg[:, 0:128]), "gc")
+    w(P, "xc2")
+    ev(P.matmul(T.psl[:, 0:256:2], T.xsb[:, 256:384], T.eye[:, :], True, True), "pd")
+    ev(P.matmul(T.psl[:, 1:256:2], T.xsb[:, 384:512], T.eye[:, :], True, True), "pd")
+
+    pairs = [("Fe", "Fo"), ("O1", "O2"), ("O0", "Dc"), ("Dr", None)]
+    w(V, "gc")
+    w(V, "tabl")
+    w(C, "gc")
+    w(C, "tabl")
+
+    def place(k):
+        if k is None:
+            return a, T.land[:, a, 0:CAP], T.land[:, a, CAP:MW]
+        return by[k], T.msg[:, by[k], 0:CAP], T.msg[:, by[k], CAP:MW]
+
+    nsent = 0
+    for n, (kv, kc2) in enumerate(pairs):
+        b0, o0, t0 = place(kv)
+        b1, o1, t1 = place(kc2)
+        gp = "gp%d" % n
+        ev(C.activation(o1, T.tabw[:, PAD:PAD + R].indirect(T.g16[:, 16 * b1:16 * b1 + 16]), F.Copy), gp)
+        if n == 0:
+            ev(V.tensor_copy(out=o0, in_=T.tabw[:, PAD:PAD + R].indirect(T.g16[:, 16 * b0:16 * b0 + 16])), gp)
+            w(V, "pd")
+        ev(V.tensor_tensor(out=t0, in0=T.psl[:, 32 * b0:32 * b0 + 32], in1=T.dtr[:, :], op=A.max), gp)
+        ev(V.tensor_tensor(out=t1, in0=T.psl[:, 32 * b1:32 * b1 + 32], in1=T.dtr[:, :], op=A.max), gp)
+        if n:
+            ev(V.tensor_copy(out=o0, in_=T.tabw[:, PAD:PAD + R].indirect(T.g16[:, 16 * b0:16 * b0 + 16])), gp)
+        w(g, gp)
+        trs = []
+        ks = [k for k in (kv, kc2) if k is not None]
+        for x, k in enumerate(ks):
+            b = by[k]
+            rid, pid = topo.addr(first[b], core)
+            trs.append(RemoteDMATransfer(dst_ids=[DstId(rid=rid, pnc=pid)], dma_engine_mask=half[x] if len(ks) == 2 else off_mask,
+                                         remote_sem=S["da%d" % a], srcs=[T.msg[:, b, :]], dsts=[T.land[:, a, :]]))
+        g.remote_dma_fused(trs, local_sem=S["dsent"])
+        nsent += len(eng)
+    g.wait_ge(S["dsent"], nsent)
+
+    for n in range(4):
+        w(V, "gp%d" % n)
+    prev = [None]
+    need = {"Dr": 8, "Dc": 4}
+    for k in (None, "Dc", "Dr", "Fe", "Fo", "O1", "O2", "O0"):
+        s = a if k is None else frm[k]
+        if k is not None:
+            V.wait_ge(S["da%d" % s], need.get(k, 8))
+        c = slice(16 * s, 16 * s + 16)
+        ev(V.tensor_tensor(out=T.dsum[:, c], in0=T.land[:, s, CAP:MW:2], in1=T.land[:, s, CAP + 1:MW:2], op=A.add), "db%d" % s)
+        w(V, "db%d" % s)
+        ev(V.tensor_copy(out=T.dof[:, c], in_=T.dsum[:, c]), "dc%d" % s)
+        w(V, "dc%d" % s)
+        if prev[0]:
+            w(V, prev[0])
+        ev(V.tensor_copy(out=T.tabw[:, 0:PAD + R].indirect(T.dof[:, c]), in_=T.land[:, s, 0:CAP]), "de%d" % s)
+        prev[0] = "de%d" % s
+    w(Y, prev[0])
+    w(C, prev[0])
+    ev(Y.dma_start(T.y[0:64, :], T.tabw[0:64, PAD:PAD + R]), "ysy", 16)
+    ev(C.dma_start(T.y[64:128, :], T.tabw[64:128, PAD:PAD + R]), "ysc", 16)
+    w(Y, "ysy")
+    w(C, "ysc")

@@ -1,8 +1,7 @@
 from concourse.bass import DstId, RemoteDMATransfer
-from concourse.mybir import dt, AluOpType as A, ActivationFunctionType as F
+from concourse.mybir import AluOpType as A, ActivationFunctionType as F
 
 N, R, CAP = 8, 4096, 256
-MW = CAP + 32
 PAD = 384
 SLOT0 = 1153
 WIN = SLOT0 + N * CAP
@@ -11,15 +10,14 @@ LW = 96
 SCRATCH = {
     "ki": ("sbuf", [128, 1], "int32"),
     "xi": ("sbuf", [128, 256], "int32"),
-    "ti": ("sbuf", [128, 16], "int32"),
+    "ti": ("sbuf", [128, 16], "float32"),
     "tr": ("sbuf", [128, 64], "float32"),
     "kb": ("sbuf", [128, 4], "int32"),
     "kf": ("sbuf", [128, 8], "float32"),
-    "kc": ("sbuf", [128, 8], "float32"),
+    "kc": ("sbuf", [128, 16], "float32"),
     "x15": ("sbuf", [128, 128], "int32"),
     "xs4": ("sbuf", [128, 128], "int32"),
-    "xs3": ("sbuf", [128, 32], "int32"),
-    "th": ("sbuf", [128, 32], "int32"),
+    "xs3": ("sbuf", [128, 16], "int32"),
     "rep": ("sbuf", [128, 128], "bfloat16"),
     "eye": ("sbuf", [128, 128], "bfloat16"),
     "za": ("sbuf", [128, 240], "bfloat16"),
@@ -28,8 +26,10 @@ SCRATCH = {
     "lb": ("sbuf", [128, 128], "float32"),
     "ltri": ("sbuf", [128, 128], "float32"),
     "gx": ("sbuf", [128, 144], "bfloat16"),
-    "wr": ("sbuf", [128, 32], "bfloat16"),
-    "dtr": ("sbuf", [128, 32], "bfloat16"),
+    "wr": ("sbuf", [128, 16], "bfloat16"),
+    "wd": ("sbuf", [128, 2], "bfloat16"),
+    "jl": ("sbuf", [128, 256], "bfloat16"),
+    "cown": ("sbuf", [128, 256], "float32"),
     "ld": ("sbuf", [128, 128], "int32"),
     "dg": ("sbuf", [128, 384], "int32"),
     "xb": ("sbuf", [128, 320], "bfloat16"),
@@ -44,12 +44,16 @@ SCRATCH = {
     "offs": ("sbuf", [128, 64], "uint16"),
     "win": ("sbuf", [128, WIN + 7], "bfloat16"),
     "xsb": ("sbuf", [128, 512], "bfloat16"),
+    "xz": ("sbuf", [128, 480], "bfloat16"),
     "g16": ("sbuf", [128, 128], "uint16"),
-    "tabw": ("sbuf", [128, PAD + R], "bfloat16"),
-    "msg": ("sbuf", [128, N, MW], "bfloat16"),
-    "land": ("sbuf", [128, N, MW], "bfloat16"),
-    "dsum": ("sbuf", [128, 128], "int32"),
-    "dof": ("sbuf", [128, 128], "uint16"),
+    "dsf": ("sbuf", [128, 16], "float32"),
+    "dof": ("sbuf", [128, 16], "uint16"),
+    "jwin": ("sbuf", [128, PAD + R], "bfloat16"),
+    "jf": ("sbuf", [128, 256], "float32"),
+    "jo": ("sbuf", [128, 256], "uint16"),
+    "big": ("sbuf", [128, R + N * CAP], "bfloat16"),
+    "msg": ("sbuf", [128, N * CAP], "bfloat16"),
+    "yb": ("sbuf", [128, R], "bfloat16"),
     "psl": ("psum", [128, 512], "float32"),
     "pss": ("psum", [128, 512], "float32"),
     "psb": ("psum", [128, 512], "float32"),
@@ -59,20 +63,24 @@ SCRATCH = {
     "psg": ("psum", [128, 512], "float32"),
 }
 _EV = ["io1", "io2", "c1", "c2", "c3", "lds", "ldd", "lo", "lx", "lp", "lready", "k1", "k2", "k3", "tabl",
-       "mrow", "scn", "tt", "bas", "ee", "em", "po", "mx", "of", "lnp", "lnc", "wz", "sc", "x1", "xc1", "xc2",
-       "pg", "gc", "pd", "ysy", "ysc"]
-SEMAPHORES = (_EV + ["gp%d" % k for k in range(4)] + ["da%d" % k for k in range(N)] + ["db%d" % k for k in range(N)]
-              + ["dc%d" % k for k in range(N)] + ["de%d" % k for k in range(N)]
-              + ["lar0", "lar1", "lsent", "dsent", "fsent"])
+       "mrow", "scn", "tt", "bas", "ee", "em", "po", "mx", "of", "lnp", "lnc", "sc", "x1", "xc1",
+       "pg", "gc", "dx", "dm", "js", "jx0", "jx1", "jc0", "jc1", "jp0", "jp1", "jm0", "jm1", "jr0", "jr1"]
+SEMAPHORES = (_EV + ["gp%d" % k for k in range(4)] + ["l%d" % k for k in range(N)] + ["yg%d" % k for k in range(4)]
+              + ["lar1", "lsent", "dsent", "fsent", "dr", "dar", "ja0", "ja1", "jsent", "ys"])
 
 
 def _chip_cores(core, topo):
     return [c for c in range(128 * topo.host(core), 128 * topo.host(core) + 128) if topo.chip(c) == topo.chip(core)]
 
 
+def _bits(m):
+    return [i for i in range(16) if (m >> i) & 1]
+
+
 def _routes(T, topo):
     cores = T.cores
     kind, relay, used = {}, {}, set(cores)
+    helper = {}
 
     def take(near, dst, other_die):
         cand = [c for c in _chip_cores(near, topo) if c not in used and topo.may_write(c, dst)]
@@ -97,6 +105,8 @@ def _routes(T, topo):
                 same = topo.chip(cores[a]) == topo.chip(cores[b])
                 kind[(a, b)] = "Fe" if same else "Fo"
                 relay[(a, b)] = take(cores[nb["Dr" if same else "Dc"]], cores[b], same)
+                if same:
+                    helper[nb["Dr"]] = relay[(a, b)]
     for a in range(n):
         for b in range(n):
             if a != b and (a, b) not in kind:
@@ -108,44 +118,50 @@ def _routes(T, topo):
                 else:
                     kind[(a, b)] = "O2"
                 relay[(a, b)] = take(ca, cb, True)
-    return kind, relay
+    return kind, relay, helper
 
 
 _CACHE = {}
 
 
-def _bits(m):
-    return [i for i in range(16) if (m >> i) & 1]
-
-
 def rank_program(g, core, T, topo):
     if "r" not in _CACHE:
         _CACHE["r"] = _routes(T, topo)
-    kind, relay = _CACHE["r"]
-    S = T.sem
+    kind, relay, helper = _CACHE["r"]
     rank = T.rank_of(core)
-    if rank is None:
-        for (a, b), c in relay.items():
-            if c == core:
-                _relay(g, core, T, topo, a, b)
-        return
-    _rank(g, core, rank, T, topo, kind, relay)
+    if rank is not None:
+        return _program(g, core, rank, True, T, topo, kind, relay, helper)
+    for a, c in helper.items():
+        if c == core:
+            return _program(g, core, a, False, T, topo, kind, relay, helper)
+    for (a, b), c in relay.items():
+        if c == core:
+            _list_on(g, core, a, b, T, topo, helper)
+            _data_on(g, core, a, b, T, topo)
+            g.wait_ge(T.sem["fsent"], 2 * len(_bits(topo.mask(core, T.cores[b]))))
 
 
-def _relay(g, core, T, topo, a, b):
+def _list_on(g, core, a, b, T, topo, helper):
     S = T.sem
-    dst = T.cores[b]
-    rid, pid = topo.addr(dst, core)
-    m = topo.mask(core, dst)
-    nm = len(_bits(m))
-    g.wait_ge(S["lar0"], 8)
-    g.remote_dma(T.lists[:, a, :], T.lists[:, a, :], S["lar1"], S["fsent"], pid, rid, m)
-    g.wait_ge(S["da%d" % a], 4)
-    g.remote_dma(T.land[:, a, :], T.land[:, a, :], S["da%d" % a], S["fsent"], pid, rid, m)
-    g.wait_ge(S["fsent"], 2 * nm)
+    dst = [T.cores[b], helper[b]]
+    ids = []
+    for c in dst:
+        rid, pid = topo.addr(c, core)
+        ids.append(DstId(rid=rid, pnc=pid))
+    g.wait_ge(S["l%d" % a], 8)
+    g.remote_dma_fused([RemoteDMATransfer(dst_ids=ids, dma_engine_mask=topo.mask(core, dst[0]), remote_sem=S["lar1"],
+                                          srcs=[T.lists[:, a, :]], dsts=[T.lists[:, a, :]] * 2)], local_sem=S["fsent"])
 
 
-def _rank(g, core, a, T, topo, kind, relay):
+def _data_on(g, core, a, b, T, topo):
+    S = T.sem
+    rid, pid = topo.addr(T.cores[b], core)
+    slot = T.big[:, R + CAP * a:R + CAP * a + CAP]
+    g.wait_ge(S["dr"], 4)
+    g.remote_dma(slot, slot, S["dar"], S["fsent"], pid, rid, topo.mask(core, T.cores[b]))
+
+
+def _program(g, core, a, sender, T, topo, kind, relay, helper):
     S = T.sem
     V, P, C, Y = g.vector, g.tensor, g.scalar, g.sync
     cnt = {}
@@ -157,26 +173,31 @@ def _rank(g, core, a, T, topo, kind, relay):
     def w(q, name):
         q.wait_ge(S[name], cnt[name])
 
-    by = {kind[(a, b)]: b for b in range(N) if b != a}
-    frm = {kind[(s, a)]: s for s in range(N) if s != a}
-    first = {b: (T.cores[b] if relay[(a, b)] is None else relay[(a, b)]) for b in range(N) if b != a}
-    order = ["Fe", "Fo", "O1", "O2", "O0", "Dc", "Dr"]
-    off_mask = topo.mask(core, first[by["Dr"]])
-    eng = _bits(off_mask)
-    half = [sum(1 << e for e in eng[:4]), sum(1 << e for e in eng[4:])]
-
-    ev(Y.dma_start(T.ld[0:16, 0:64], T.src[:, :]), "lds", 16)
-    ev(C.dma_start(T.ld[0:16, 64:128], T.dst[:, :]), "ldd", 16)
-    ev(g.iota(T.ki[:, :], [[1, 1]], 0, 1), "io1")
-    ev(g.iota(T.xi[:, :], [[1, 256]], 0, 0), "io1")
-    ev(g.iota(T.ti[:, :], [[16, 16]], 0, 1), "io2")
-    ev(g.iota(T.tr[:, :], [[16, 64]], 0, 1, allow_small_or_imprecise_dtypes=True), "io2")
-
     def ts(out, in0, s1, s2, op0, op1=None):
         if op1 is None:
             return V.tensor_scalar(out=out, in0=in0, scalar1=s1, scalar2=None, op0=op0)
         return V.tensor_scalar(out=out, in0=in0, scalar1=s1, scalar2=s2, op0=op0, op1=op1)
 
+    by = {kind[(a, b)]: b for b in range(N) if b != a}
+    frm = {kind[(s, a)]: s for s in range(N) if s != a}
+    first = {b: (T.cores[b] if relay[(a, b)] is None else relay[(a, b)]) for b in range(N) if b != a}
+    off_mask = topo.mask(core, first[by["Dr"]])
+    eng = _bits(off_mask)
+    half = [sum(1 << e for e in eng[:4]), sum(1 << e for e in eng[4:])]
+
+    if sender:
+        ev(Y.dma_start(T.ld[0:16, 0:64], T.src[:, :]), "lds", 16)
+        ev(C.dma_start(T.ld[0:16, 64:128], T.dst[:, :]), "ldd", 16)
+    ev(g.iota(T.ki[:, :], [[1, 1]], 0, 1), "io1")
+    ev(g.iota(T.xi[:, :], [[1, 256]], 0, 0), "io1")
+    ev(g.iota(T.tr[:, :], [[16, 64]], 0, 1, allow_small_or_imprecise_dtypes=True), "io2")
+    if not sender:
+        ev(g.iota(T.ti[:, :], [[16, 16]], 0, 1, allow_small_or_imprecise_dtypes=True), "io2")
+        served = [ab for ab in relay if relay[ab] == core][0]
+        _list_on(g, core, served[0], served[1], T, topo, helper)
+        _data_on(g, core, served[0], served[1], T, topo)
+
+    kf, kc = T.kf, T.kc
     w(V, "io1")
     ev(ts(T.kb[:, 0:1], T.ki[:, :], 15, None, A.bitwise_and), "c1")
     ev(ts(T.kb[:, 1:2], T.ki[:, :], 4, None, A.arith_shift_right), "c1")
@@ -184,89 +205,104 @@ def _rank(g, core, a, T, topo, kind, relay):
     ev(ts(T.kb[:, 3:4], T.ki[:, :], 5, None, A.arith_shift_right), "c1")
     ev(ts(T.x15[:, :], T.xi[:, 0:128], 15, None, A.bitwise_and), "c1")
     w(V, "c1")
-    ev(V.tensor_copy(out=T.kf[:, 0:4], in_=T.kb[:, :]), "c2")
-    ev(V.tensor_copy(out=T.kf[:, 4:5], in_=T.ki[:, :]), "c2")
+    ev(V.tensor_copy(out=kf[:, 0:4], in_=T.kb[:, :]), "c2")
+    ev(V.tensor_copy(out=kf[:, 4:5], in_=T.ki[:, :]), "c2")
     w(V, "c2")
-    ev(ts(T.rep[0:16, :], T.x15[0:16, :], T.kf[0:16, 4:5], None, A.is_equal), "c3")
-    ev(ts(T.eye[:, :], T.xi[:, 0:128], T.kf[:, 4:5], None, A.is_equal), "c3")
+    ev(ts(T.rep[0:16, :], T.x15[0:16, :], kf[0:16, 4:5], None, A.is_equal), "c3")
+    ev(ts(T.eye[:, :], T.xi[:, 0:128], kf[:, 4:5], None, A.is_equal), "c3")
 
-    w(V, "lds")
-    w(V, "ldd")
-    src, dst = T.ld[0:16, 0:64], T.ld[0:16, 64:128]
-    d = lambda k: T.dg[0:16, 64 * k:64 * k + 64]
-    ev(ts(d(0), src, 0xF000, None, A.bitwise_and), "lo")
-    ev(ts(d(1), dst, 3, 0x1E00, A.arith_shift_right, A.bitwise_and), "lo")
-    ev(ts(d(2), src, 4032, None, A.bitwise_and), "lo")
-    ev(ts(d(3), src, 63, None, A.bitwise_and), "lo")
-    ev(ts(d(4), dst, 4064, None, A.bitwise_and), "lo")
-    ev(ts(d(5), dst, 31, None, A.bitwise_and), "lo")
-    w(V, "lo")
-    ev(V.tensor_tensor(out=T.xb[0:16, 0:64], in0=d(0), in1=d(1), op=A.add), "lx")
-    ev(V.tensor_copy(out=T.xb[0:16, 64:192], in_=T.dg[0:16, 128:256]), "lx")
-    ev(ts(T.xb[0:16, 192:256], d(4), float(PAD - 32), None, A.add), "lx")
-    ev(ts(T.xb[0:16, 256:320], d(5), 32.0, None, A.add), "lx")
-    w(P, "c3")
-    w(P, "lx")
-    ev(P.matmul(T.psl[:, 0:64], T.rep[0:16, :], T.xb[0:16, 0:64], True, True), "lp")
-    ev(P.matmul(T.psl[:, 64:80], T.xb[0:16, 64:320:2], T.eye[0:16, 0:16], True, True), "lp")
-    ev(P.matmul(T.psl[:, 80:96], T.xb[0:16, 65:320:2], T.eye[0:16, 0:16], True, True), "lp")
-    w(V, "lp")
-    ev(V.tensor_copy(out=T.lists[:, a, :], in_=T.psl[:, 0:96]), "lready")
+    if sender:
+        w(V, "lds")
+        w(V, "ldd")
+        src, dst = T.ld[0:16, 0:64], T.ld[0:16, 64:128]
+        d = lambda k: T.dg[0:16, 64 * k:64 * k + 64]
+        ev(ts(d(0), src, 0xF000, None, A.bitwise_and), "lo")
+        ev(ts(d(1), dst, 3, 0x1E00, A.arith_shift_right, A.bitwise_and), "lo")
+        ev(ts(d(2), src, 4032, None, A.bitwise_and), "lo")
+        ev(ts(d(3), src, 63, None, A.bitwise_and), "lo")
+        ev(ts(d(4), dst, 4064, None, A.bitwise_and), "lo")
+        ev(ts(d(5), dst, 31, None, A.bitwise_and), "lo")
+        w(V, "lo")
+        ev(V.tensor_tensor(out=T.xb[0:16, 0:64], in0=d(0), in1=d(1), op=A.add), "lx")
+        ev(V.tensor_copy(out=T.xb[0:16, 64:192], in_=T.dg[0:16, 128:256]), "lx")
+        ev(ts(T.xb[0:16, 192:256], d(4), float(PAD), None, A.add), "lx")
+        ev(V.tensor_copy(out=T.xb[0:16, 256:320], in_=d(5)), "lx")
+        w(P, "c3")
+        w(P, "lx")
+        ev(P.matmul(T.psl[:, 0:64], T.rep[0:16, :], T.xb[0:16, 0:64], True, True), "lp")
+        ev(P.matmul(T.psl[:, 64:80], T.xb[0:16, 64:320:2], T.eye[0:16, 0:16], True, True), "lp")
+        ev(P.matmul(T.psl[:, 80:96], T.xb[0:16, 65:320:2], T.eye[0:16, 0:16], True, True), "lp")
+        w(V, "lp")
+        ev(V.tensor_copy(out=T.lists[:, a, :], in_=T.psl[:, 0:96]), "lready")
 
-    w(g, "lready")
-    ids, outs = [], []
-    for k in order:
-        rid, pid = topo.addr(first[by[k]], core)
-        ids.append(DstId(rid=rid, pnc=pid))
-        outs.append(T.lists[:, a, :])
-    g.remote_dma_fused([RemoteDMATransfer(dst_ids=ids, dma_engine_mask=off_mask, remote_sem=S["lar0"],
-                                          srcs=[T.lists[:, a, :]], dsts=outs)], local_sem=S["lsent"])
-    Y.wait_ge(S["lsent"], len(eng))
-    ev(Y.dma_start(T.tabw[:, PAD:PAD + R], T.tab[:, :]), "tabl", 16)
+        w(g, "lready")
+        dests = [first[by[k]] for k in ("Fe", "Fo", "O1", "O2", "O0", "Dc", "Dr")]
+        dests += [c for c in (helper[by["Dc"]], helper[by["Dr"]], helper[a]) if c not in dests]
+        ids = []
+        for c in dests:
+            rid, pid = topo.addr(c, core)
+            ids.append(DstId(rid=rid, pnc=pid))
+        g.remote_dma_fused([RemoteDMATransfer(dst_ids=ids, dma_engine_mask=off_mask, remote_sem=S["l%d" % a],
+                                              srcs=[T.lists[:, a, :]], dsts=[T.lists[:, a, :]] * len(ids))], local_sem=S["lsent"])
+        Y.wait_ge(S["lsent"], len(eng))
+        ev(Y.dma_start(T.big[:, 0:R], T.tab[:, :]), "tabl", 16)
 
     w(V, "c3")
     w(V, "io2")
-    kf, kc = T.kf, T.kc
-    ev(ts(kc[:, 0:1], kf[:, 1:2], 512.0, 4096.0 * a, A.mult, A.add), "k1")
+    if sender:
+        ev(ts(kc[:, 0:1], kf[:, 1:2], 512.0, 4096.0 * a, A.mult, A.add), "k1")
+    else:
+        ev(ts(kc[:, 0:1], kf[:, 1:2], 4096.0, 512.0 * a, A.mult, A.add), "k1")
     ev(ts(kc[:, 1:2], kf[:, 1:2], 256.0, float(SLOT0 - 1), A.mult, A.add), "k1")
     ev(ts(kc[:, 2:3], kf[:, 2:3], 4.0, None, A.mult), "k1")
     ev(ts(T.xs4[:, :], T.xi[:, 0:128], 4, None, A.arith_shift_right), "k1")
-    ev(ts(T.xs3[:, :], T.xi[:, 0:32], 3, None, A.arith_shift_right), "k1")
-    ev(ts(T.th[:, 0:16], T.ti[:, :], 0x7FE0, None, A.bitwise_and), "k1")
-    ev(ts(T.th[:, 16:32], T.ti[:, :], 31, None, A.bitwise_and), "k1")
+    ev(ts(T.xs3[:, :], T.xi[:, 0:16], 3, None, A.arith_shift_right), "k1")
     ev(V.memset(T.za[:, :], 0.0), "k1")
     ev(V.memset(T.zc[:, :], 0.0), "k1")
     ev(ts(T.lb[:, :], T.xi[:, 0:128], kf[:, 4:5], None, A.is_gt), "k1")
+    if not sender:
+        ev(ts(kc[:, 4:5], kf[:, 0:1], -2.0, None, A.add), "k1")
+        ev(ts(kc[:, 5:6], kf[:, 0:1], 1.0, None, A.is_equal), "k1")
+        ev(ts(kc[:, 6:7], kf[:, 0:1], 0.0, None, A.is_equal), "k1")
+        ev(ts(kc[:, 7:8], kf[:, 1:2], 256.0, float(R), A.mult, A.add), "k1")
+        ev(V.memset(T.xz[:, :], 0.0), "k1")
     w(V, "k1")
     ev(V.tensor_tensor(out=kc[:, 3:4], in0=kc[:, 2:3], in1=kf[:, 3:4], op=A.add), "k2")
     ev(ts(T.la[:, :], T.xs4[:, :], kf[:, 1:2], None, A.is_equal), "k2")
+    if not sender:
+        ev(V.tensor_tensor(out=kc[:, 8:9], in0=kc[:, 6:7], in1=kc[:, 7:8], op=A.mult), "k2")
     w(V, "k2")
     ev(V.tensor_tensor(out=T.ltri[:, :], in0=T.la[:, :], in1=T.lb[:, :], op=A.mult), "k3")
     ev(ts(T.gx[:, :], T.xi[:, 0:144], kc[:, 3:4], None, A.is_equal), "k3")
     ev(ts(T.wr[:, :], T.xs3[:, :], kf[:, 0:1], None, A.is_equal), "k3")
     ev(ts(T.za[:, 112:128], T.xi[:, 0:16], kf[:, 0:1], None, A.is_equal), "k3")
     ev(ts(T.zc[:, 112:128], T.xi[:, 0:16], kf[:, 0:1], kc[:, 1:2], A.is_equal, A.mult), "k3")
-    ev(V.tensor_copy(out=T.dtr[:, 0:32:2], in_=T.th[:, 0:16]), "k3")
-    ev(V.tensor_copy(out=T.dtr[:, 1:32:2], in_=T.th[:, 16:32]), "k3")
     ev(V.memset(T.win[:, SLOT0:WIN], 0.0), "k3")
+    if not sender:
+        ev(ts(T.wd[:, :], T.xi[:, 0:2], kc[:, 4:5], None, A.is_equal), "k3")
+        ev(ts(T.jl[:, :], T.xi[:, :], kc[:, 5:6], kc[:, 8:9], A.mult, A.add), "k3")
+        ev(ts(T.cown[:, :], T.xi[:, :], 16.0, kf[:, 0:1], A.mult, A.add), "k3")
+        ev(V.memset(T.jwin[:, PAD:PAD + R], 0.0), "k3")
     w(V, "k3")
 
     def mrow(r):
         ev(ts(T.mm[:, r:512:8], T.lists[:, r, 0:64], kc[:, 0:1], None, A.is_equal), "mrow")
 
-    mrow(a)
-    V.wait_ge(S["lar0"], 16)
-    mrow(frm["Dr"])
-    mrow(frm["Dc"])
+    w(P, "k3")
+    for k in (None, "Dr", "Dc"):
+        s = a if k is None else frm[k]
+        if k is None and sender:
+            w(P, "lready")
+        else:
+            V.wait_ge(S["l%d" % s], 8)
+            P.wait_ge(S["l%d" % s], 8)
+        mrow(s)
     V.wait_ge(S["lar1"], 40)
+    P.wait_ge(S["lar1"], 40)
     for k in ("Fe", "Fo", "O0", "O1", "O2"):
         mrow(frm[k])
     w(V, "mrow")
     ev(V.tensor_tensor_scan(out=T.pss[:, :], data0=T.mm[:, :], data1=T.mm[:, :], initial=0.0, op0=A.add, op1=A.max), "scn")
-    w(P, "k3")
-    w(P, "lready")
-    P.wait_ge(S["lar0"], 16)
-    P.wait_ge(S["lar1"], 40)
     for s in range(4):
         for e in range(2):
             j = 2 * s + e
@@ -300,77 +336,109 @@ def _rank(g, core, a, T, topo, kind, relay):
     w(V, "lnc")
     ev(V.tensor_copy(out=T.win[:, 0:WIN].indirect(T.offs[:, 0:64]), in_=T.lin[:, :]), "sc")
     w(P, "sc")
+    wslot = lambda i: T.win[:, SLOT0 + i:SLOT0 + i + 2033:16]
+
+    if not sender:
+        for i in range(16):
+            ev(P.matmul(T.psx[:, i:32:16], wslot(i), T.wd[:, :], True, True), "x1")
+        w(V, "x1")
+        ev(V.tensor_copy(out=T.xz[:, 112:128], in_=T.psx[:, 0:16]), "dx")
+        ev(V.tensor_copy(out=T.xz[:, 352:368], in_=T.psx[:, 16:32]), "dx")
+        w(P, "dx")
+        for s in range(N):
+            for d in (0, 240):
+                i = P.matmul(T.psg[:, 0:16], T.xz[:, d + 112 - 16 * s:d + 240 - 16 * s], T.eye[:, 16 * s:16 * s + 16],
+                             s == 0 and d == 0, s == N - 1 and d == 240)
+        ev(i, "pg")
+        w(V, "pg")
+        ev(V.tensor_tensor(out=T.dsf[:, :], in0=T.psg[:, 0:16], in1=T.ti[:, :], op=A.max), "dm")
+        w(V, "dm")
+        ev(V.tensor_copy(out=T.dof[:, :], in_=T.dsf[:, :]), "gc")
+        w(V, "gc")
+        ev(V.tensor_copy(out=T.jwin[:, 0:PAD + R].indirect(T.dof[:, 0:16]), in_=T.jl[:, :]), "js")
+        w(P, "js")
+        to = [T.pss, T.pso]
+        for h in range(2):
+            b0 = PAD + 2048 * h
+            for i in range(16):
+                ev(P.matmul(T.psn[:, 512 * h + i:512 * h + 256:16], T.jwin[:, b0 + i:b0 + i + 2033:16], T.wr[:, :], True, True), "jx%d" % h)
+            x0 = 256 * h
+            if h == 0:
+                w(V, "jx0")
+                ev(V.tensor_copy(out=T.xsb[:, 0:256], in_=T.psn[:, 0:256]), "jc0")
+            else:
+                w(C, "jx1")
+                ev(C.activation(T.xsb[:, 256:512], T.psn[:, 512:768], F.Copy), "jc1")
+            w(P, "jc%d" % h)
+            P.matmul(to[h][:, 0:128], T.xsb[:, x0:x0 + 128], T.eye[:, :], True, False)
+            ev(P.matmul(to[h][:, 0:128], T.xsb[:, x0 + 128:x0 + 256], T.eye[:, :], False, True), "jp%d" % h)
+            j = slice(128 * h, 128 * h + 128)
+            w(V, "jp%d" % h)
+            ev(V.tensor_tensor(out=T.jf[:, j], in0=to[h][:, 0:128], in1=T.cown[:, j], op=A.max), "jm%d" % h)
+            w(V, "jm%d" % h)
+            ev(V.tensor_copy(out=T.jo[:, j], in_=T.jf[:, j]), "jr%d" % h)
+            w(g, "jr%d" % h)
+            rid, pid = topo.addr(T.cores[a], core)
+            g.remote_dma(T.jo[:, j], T.jo[:, j], S["ja%d" % h], S["jsent"], pid, rid, off_mask)
+        g.wait_ge(S["jsent"], 2 * len(eng))
+        g.wait_ge(S["fsent"], 2 * len(eng))
+        return
+
     for i in range(16):
-        ev(P.matmul(T.psx[:, i:512:16], T.win[:, SLOT0 + i:SLOT0 + i + 2033:16], T.wr[:, :], True, True), "x1")
+        ev(P.matmul(T.psx[:, i:256:16], wslot(i), T.wr[:, :], True, True), "x1")
     w(V, "x1")
     ev(V.tensor_copy(out=T.xsb[:, 0:256], in_=T.psx[:, 0:256]), "xc1")
     w(P, "xc1")
     P.matmul(T.psg[:, 0:128], T.xsb[:, 0:128], T.eye[:, :], True, False)
     ev(P.matmul(T.psg[:, 0:128], T.xsb[:, 128:256], T.eye[:, :], False, True), "pg")
-    w(C, "xc1")
-    ev(C.activation(T.xsb[:, 256:512], T.psx[:, 256:512], F.Copy), "xc2")
     w(V, "pg")
     ev(V.tensor_copy(out=T.g16[:, :], in_=T.psg[:, 0:128]), "gc")
-    w(P, "xc2")
-    ev(P.matmul(T.psl[:, 0:256:2], T.xsb[:, 256:384], T.eye[:, :], True, True), "pd")
-    ev(P.matmul(T.psl[:, 1:256:2], T.xsb[:, 384:512], T.eye[:, :], True, True), "pd")
 
     pairs = [("Fe", "Fo"), ("O1", "O2"), ("O0", "Dc"), ("Dr", None)]
-    w(V, "gc")
-    w(V, "tabl")
-    w(C, "gc")
-    w(C, "tabl")
+    for q in (V, C):
+        w(q, "gc")
+        w(q, "tabl")
+    own = slice(R + CAP * a, R + CAP * a + CAP)
+
+    def gat(q, out, win, off, name):
+        if q is V:
+            ev(V.tensor_copy(out=out, in_=win.indirect(off)), name)
+        else:
+            ev(C.activation(out, win.indirect(off), F.Copy, bias=-0.0), name)
 
     def place(k):
         if k is None:
-            return a, T.land[:, a, 0:CAP], T.land[:, a, CAP:MW]
-        return by[k], T.msg[:, by[k], 0:CAP], T.msg[:, by[k], CAP:MW]
+            return a, T.big[:, own]
+        return by[k], T.msg[:, CAP * by[k]:CAP * by[k] + CAP]
 
     nsent = 0
-    for n, (kv, kc2) in enumerate(pairs):
-        b0, o0, t0 = place(kv)
-        b1, o1, t1 = place(kc2)
-        gp = "gp%d" % n
-        ev(C.activation(o1, T.tabw[:, PAD:PAD + R].indirect(T.g16[:, 16 * b1:16 * b1 + 16]), F.Copy), gp)
-        if n == 0:
-            ev(V.tensor_copy(out=o0, in_=T.tabw[:, PAD:PAD + R].indirect(T.g16[:, 16 * b0:16 * b0 + 16])), gp)
-            w(V, "pd")
-        ev(V.tensor_tensor(out=t0, in0=T.psl[:, 32 * b0:32 * b0 + 32], in1=T.dtr[:, :], op=A.max), gp)
-        ev(V.tensor_tensor(out=t1, in0=T.psl[:, 32 * b1:32 * b1 + 32], in1=T.dtr[:, :], op=A.max), gp)
-        if n:
-            ev(V.tensor_copy(out=o0, in_=T.tabw[:, PAD:PAD + R].indirect(T.g16[:, 16 * b0:16 * b0 + 16])), gp)
-        w(g, gp)
+    for n, pr in enumerate(pairs):
+        for q, k in zip((V, C), pr):
+            b, out = place(k)
+            gat(q, out, T.big[:, 0:R], T.g16[:, 16 * b:16 * b + 16], "gp%d" % n)
+        w(g, "gp%d" % n)
         trs = []
-        ks = [k for k in (kv, kc2) if k is not None]
+        ks = [k for k in pr if k is not None]
         for x, k in enumerate(ks):
             b = by[k]
             rid, pid = topo.addr(first[b], core)
             trs.append(RemoteDMATransfer(dst_ids=[DstId(rid=rid, pnc=pid)], dma_engine_mask=half[x] if len(ks) == 2 else off_mask,
-                                         remote_sem=S["da%d" % a], srcs=[T.msg[:, b, :]], dsts=[T.land[:, a, :]]))
+                                         remote_sem=S["dar" if relay[(a, b)] is None else "dr"],
+                                         srcs=[place(k)[1]], dsts=[T.big[:, own]]))
         g.remote_dma_fused(trs, local_sem=S["dsent"])
         nsent += len(eng)
     g.wait_ge(S["dsent"], nsent)
 
+    for q in (V, C):
+        w(q, "gp3")
+        q.wait_ge(S["dar"], 5 * 8 + 8 + 4)
+        q.wait_ge(S["ja0"], 8)
     for n in range(4):
-        w(V, "gp%d" % n)
-    prev = [None]
-    need = {"Dr": 8, "Dc": 4}
-    for k in (None, "Dc", "Dr", "Fe", "Fo", "O1", "O2", "O0"):
-        s = a if k is None else frm[k]
-        if k is not None:
-            V.wait_ge(S["da%d" % s], need.get(k, 8))
-        c = slice(16 * s, 16 * s + 16)
-        ev(V.tensor_tensor(out=T.dsum[:, c], in0=T.land[:, s, CAP:MW:2], in1=T.land[:, s, CAP + 1:MW:2], op=A.add), "db%d" % s)
-        w(V, "db%d" % s)
-        ev(V.tensor_copy(out=T.dof[:, c], in_=T.dsum[:, c]), "dc%d" % s)
-        w(V, "dc%d" % s)
-        if prev[0]:
-            w(V, prev[0])
-        ev(V.tensor_copy(out=T.tabw[:, 0:PAD + R].indirect(T.dof[:, c]), in_=T.land[:, s, 0:CAP]), "de%d" % s)
-        prev[0] = "de%d" % s
-    w(Y, prev[0])
-    w(C, prev[0])
-    ev(Y.dma_start(T.y[0:64, :], T.tabw[0:64, PAD:PAD + R]), "ysy", 16)
-    ev(C.dma_start(T.y[64:128, :], T.tabw[64:128, PAD:PAD + R]), "ysc", 16)
-    w(Y, "ysy")
-    w(C, "ysc")
+        q = (V, C)[n % 2]
+        if n == 2:
+            V.wait_ge(S["ja1"], 8)
+            C.wait_ge(S["ja1"], 8)
+        gat(q, T.yb[:, 1024 * n:1024 * n + 1024], T.big[:, :], T.jo[:, 64 * n:64 * n + 64], "yg%d" % n)
+        w(Y, "yg%d" % n)
+        ev(Y.dma_start(T.y[:, 1024 * n:1024 * n + 1024], T.yb[:, 1024 * n:1024 * n + 1024]), "ys", 16)
+    w(Y, "ys")

@@ -1,44 +1,46 @@
 from concourse.bass import DstId, RemoteDMATransfer
-from concourse.mybir import AluOpType as A, ActivationFunctionType as F
+from concourse.mybir import AluOpType as A, ActivationFunctionType as F, AxisListType as X
 
 N, R, CAP = 8, 4096, 256
 PAD = 384
 SLOT0 = 1153
 WIN = SLOT0 + N * CAP
-LW = 96
+SEG = 129
 
 SCRATCH = {
+    "lst": ("dram", [N, 128, 16], "int32"),
+    "s2": ("sbuf", [128, 128], "int32"),
+    "d2": ("sbuf", [128, 128], "int32"),
+    "sb": ("sbuf", [128, 128], "int32"),
+    "db": ("sbuf", [128, 128], "int32"),
+    "dg": ("sbuf", [128, 128], "int32"),
+    "dgb": ("sbuf", [128, 128], "bfloat16"),
+    "cls": ("sbuf", [128, 128], "bfloat16"),
     "ki": ("sbuf", [128, 1], "int32"),
     "xi": ("sbuf", [128, 256], "int32"),
     "ti": ("sbuf", [128, 16], "float32"),
     "tr": ("sbuf", [128, 64], "float32"),
-    "kb": ("sbuf", [128, 4], "int32"),
+    "kb": ("sbuf", [128, 8], "int32"),
     "kf": ("sbuf", [128, 8], "float32"),
-    "kc": ("sbuf", [128, 16], "float32"),
-    "x15": ("sbuf", [128, 128], "int32"),
-    "xs4": ("sbuf", [128, 128], "int32"),
+    "kc": ("sbuf", [128, 32], "float32"),
+    "xs6": ("sbuf", [128, 128], "int32"),
     "xs3": ("sbuf", [128, 16], "int32"),
-    "rep": ("sbuf", [128, 128], "bfloat16"),
     "eye": ("sbuf", [128, 128], "bfloat16"),
-    "za": ("sbuf", [128, 240], "bfloat16"),
-    "zc": ("sbuf", [128, 240], "bfloat16"),
+    "um": ("sbuf", [128, 144], "bfloat16"),
+    "zc": ("sbuf", [128, 4, 144], "bfloat16"),
     "la": ("sbuf", [128, 128], "float32"),
     "lb": ("sbuf", [128, 128], "float32"),
     "ltri": ("sbuf", [128, 128], "float32"),
     "gx": ("sbuf", [128, 144], "bfloat16"),
+    "seg": ("sbuf", [128, 2 * SEG], "bfloat16"),
     "wr": ("sbuf", [128, 16], "bfloat16"),
     "wd": ("sbuf", [128, 2], "bfloat16"),
     "jl": ("sbuf", [128, 256], "bfloat16"),
     "cown": ("sbuf", [128, 256], "float32"),
-    "ld": ("sbuf", [128, 128], "int32"),
-    "dg": ("sbuf", [128, 384], "int32"),
-    "xb": ("sbuf", [128, 320], "bfloat16"),
-    "lists": ("sbuf", [128, N, LW], "bfloat16"),
-    "mm": ("sbuf", [128, 512], "bfloat16"),
-    "mb": ("sbuf", [128, 512], "bfloat16"),
-    "me": ("sbuf", [128, 512], "bfloat16"),
+    "mm": ("sbuf", [128, 4 * SEG], "bfloat16"),
+    "me": ("sbuf", [128, 4 * SEG], "bfloat16"),
     "junk": ("sbuf", [128, 512], "bfloat16"),
-    "tot": ("sbuf", [128, 1], "float32"),
+    "tot": ("sbuf", [128, 4], "float32"),
     "lin": ("sbuf", [128, 1024], "bfloat16"),
     "offf": ("sbuf", [128, 64], "float32"),
     "offs": ("sbuf", [128, 64], "uint16"),
@@ -54,18 +56,19 @@ SCRATCH = {
     "big": ("sbuf", [128, R + N * CAP], "bfloat16"),
     "msg": ("sbuf", [128, N * CAP], "bfloat16"),
     "yb": ("sbuf", [128, R], "bfloat16"),
-    "psl": ("psum", [128, 512], "float32"),
-    "pss": ("psum", [128, 512], "float32"),
+    "psa": ("psum", [128, 512], "float32"),
+    "psc": ("psum", [128, 512], "float32"),
     "psb": ("psum", [128, 512], "float32"),
     "pso": ("psum", [128, 512], "float32"),
     "psn": ("psum", [128, 1024], "float32"),
     "psx": ("psum", [128, 512], "float32"),
     "psg": ("psum", [128, 512], "float32"),
 }
-_EV = ["io1", "io2", "c1", "c2", "c3", "lds", "ldd", "lo", "lx", "lp", "lready", "k1", "k2", "k3", "tabl",
-       "mrow", "scn", "tt", "bas", "ee", "em", "po", "mx", "of", "lnp", "lnc", "sc", "x1", "xc1",
+YBLK = [(0, 0, 512), (1, 512, 768), (1, 1280, 768), (0, 2048, 1024), (0, 3072, 512), (1, 3584, 512)]
+_EV = ["io1", "io2", "c1", "c2", "c3", "own", "lds", "ldd", "k1", "k2", "k3", "tabl", "sh", "cl", "m0", "m1", "m2", "m3",
+       "dl", "db2", "tt", "tr3", "bas", "inj", "sc0", "sc1", "ee0", "ee1", "po", "mx", "of", "ln0", "ln1", "lnc", "sc", "x1", "xc1",
        "pg", "gc", "dx", "dm", "js", "jx0", "jx1", "jc0", "jc1", "jp0", "jp1", "jm0", "jm1", "jr0", "jr1"]
-SEMAPHORES = (_EV + ["gp%d" % k for k in range(4)] + ["l%d" % k for k in range(N)] + ["yg%d" % k for k in range(4)]
+SEMAPHORES = (_EV + ["gp%d" % k for k in range(4)] + ["l%d" % k for k in range(N)] + ["yg%d" % k for k in range(len(YBLK))]
               + ["lar1", "lsent", "dsent", "fsent", "dr", "dar", "ja0", "ja1", "jsent", "ys"])
 
 
@@ -75,6 +78,10 @@ def _chip_cores(core, topo):
 
 def _bits(m):
     return [i for i in range(16) if (m >> i) & 1]
+
+
+def _mask(bits):
+    return sum(1 << e for e in bits)
 
 
 def _routes(T, topo):
@@ -121,6 +128,13 @@ def _routes(T, topo):
     return kind, relay, helper
 
 
+def _engines(core, a, T, topo, kind, relay, helper):
+    by = {kind[(a, b)]: b for b in range(N) if b != a}
+    off = _bits(topo.mask(T.cores[a], T.cores[by["Dr"]]))
+    on = [e for e in _bits(topo.mask(T.cores[a], helper[a])) if e not in off]
+    return off, off[:len(off) // 2], off[len(off) // 2:], on
+
+
 _CACHE = {}
 
 
@@ -136,28 +150,34 @@ def rank_program(g, core, T, topo):
             return _program(g, core, a, False, T, topo, kind, relay, helper)
     for (a, b), c in relay.items():
         if c == core:
-            _list_on(g, core, a, b, T, topo, helper)
-            _data_on(g, core, a, b, T, topo)
+            _list_on(g, core, a, b, T, topo, kind, relay, helper)
+            _data_on(g, core, a, b, T, topo, kind, relay, helper)
             g.wait_ge(T.sem["fsent"], 2 * len(_bits(topo.mask(core, T.cores[b]))))
 
 
-def _list_on(g, core, a, b, T, topo, helper):
-    S = T.sem
-    dst = [T.cores[b], helper[b]]
-    ids = []
-    for c in dst:
+def _ids(dests, core, topo):
+    out = []
+    for c in dests:
         rid, pid = topo.addr(c, core)
-        ids.append(DstId(rid=rid, pnc=pid))
-    g.wait_ge(S["l%d" % a], 8)
-    g.remote_dma_fused([RemoteDMATransfer(dst_ids=ids, dma_engine_mask=topo.mask(core, dst[0]), remote_sem=S["lar1"],
-                                          srcs=[T.lists[:, a, :]], dsts=[T.lists[:, a, :]] * 2)], local_sem=S["fsent"])
+        out.append(DstId(rid=rid, pnc=pid))
+    return out
 
 
-def _data_on(g, core, a, b, T, topo):
+def _list_on(g, core, a, b, T, topo, kind, relay, helper):
     S = T.sem
+    off, lo, hi, on = _engines(core, a, T, topo, kind, relay, helper)
+    dst = [T.cores[b], helper[b]]
+    g.wait_ge(S["l%d" % a], len(lo))
+    g.remote_dma_fused([RemoteDMATransfer(dst_ids=_ids(dst, core, topo), dma_engine_mask=topo.mask(core, dst[0]), remote_sem=S["lar1"],
+                                          srcs=[T.lst[a]], dsts=[T.lst[a]] * 2)], local_sem=S["fsent"])
+
+
+def _data_on(g, core, a, b, T, topo, kind, relay, helper):
+    S = T.sem
+    off, lo, hi, on = _engines(core, a, T, topo, kind, relay, helper)
     rid, pid = topo.addr(T.cores[b], core)
     slot = T.big[:, R + CAP * a:R + CAP * a + CAP]
-    g.wait_ge(S["dr"], 4)
+    g.wait_ge(S["dr"], len(off) + len(on) if kind[(a, b)] == "O0" else len(on) if kind[(a, b)] in ("O1", "O2") else len(off))
     g.remote_dma(slot, slot, S["dar"], S["fsent"], pid, rid, topo.mask(core, T.cores[b]))
 
 
@@ -181,152 +201,147 @@ def _program(g, core, a, sender, T, topo, kind, relay, helper):
     by = {kind[(a, b)]: b for b in range(N) if b != a}
     frm = {kind[(s, a)]: s for s in range(N) if s != a}
     first = {b: (T.cores[b] if relay[(a, b)] is None else relay[(a, b)]) for b in range(N) if b != a}
-    off_mask = topo.mask(core, first[by["Dr"]])
-    eng = _bits(off_mask)
-    half = [sum(1 << e for e in eng[:4]), sum(1 << e for e in eng[4:])]
+    off, lo, hi, on = _engines(core, a, T, topo, kind, relay, helper)
 
+    XW = 144 if sender else 256
     if sender:
-        ev(Y.dma_start(T.ld[0:16, 0:64], T.src[:, :]), "lds", 16)
-        ev(C.dma_start(T.ld[0:16, 64:128], T.dst[:, :]), "ldd", 16)
+        ev(Y.dma_start(T.lst[a, 0:64, :], T.src[:, :]), "own", 16)
+        ev(C.dma_start(T.lst[a, 64:128, :], T.dst[:, :]), "own", 16)
     ev(g.iota(T.ki[:, :], [[1, 1]], 0, 1), "io1")
-    ev(g.iota(T.xi[:, :], [[1, 256]], 0, 0), "io1")
+    ev(g.iota(T.xi[:, 0:XW], [[1, XW]], 0, 0), "io1")
+    if sender:
+        w(g, "own")
+        near = [first[by[k]] for k in ("Fe", "Fo", "O1", "O2", "O0")]
+        far = [first[by[k]] for k in ("Dc", "Dr")]
+        far += [c for c in (helper[by["Dc"]], helper[by["Dr"]]) if c not in near]
+
+        def send(parts):
+            g.remote_dma_fused([RemoteDMATransfer(dst_ids=_ids(d, core, topo), dma_engine_mask=_mask(e), remote_sem=S["l%d" % a],
+                                                  srcs=[T.lst[a]], dsts=[T.lst[a]] * len(d)) for d, e in parts], local_sem=S["lsent"])
+        send([(near, lo)])
+        send([(far, hi), ([helper[a]], on)])
     ev(g.iota(T.tr[:, :], [[16, 64]], 0, 1, allow_small_or_imprecise_dtypes=True), "io2")
     if not sender:
         ev(g.iota(T.ti[:, :], [[16, 16]], 0, 1, allow_small_or_imprecise_dtypes=True), "io2")
         served = [ab for ab in relay if relay[ab] == core][0]
-        _list_on(g, core, served[0], served[1], T, topo, helper)
-        _data_on(g, core, served[0], served[1], T, topo)
+        _list_on(g, core, served[0], served[1], T, topo, kind, relay, helper)
+        _data_on(g, core, served[0], served[1], T, topo, kind, relay, helper)
+    else:
+        Y.wait_ge(S["lsent"], len(lo) + len(hi) + len(on))
+        ev(Y.dma_start(T.big[:, 0:R], T.tab[:, :]), "tabl", 16)
+
+    for q, t, o, name in ((Y, T.s2, 0, "lds"), (C, T.d2, 64, "ldd")):
+        if sender:
+            w(q, "own")
+        else:
+            q.wait_ge(S["l%d" % a], len(on))
+        q.wait_ge(S["l%d" % frm["Dr"]], len(lo if helper[a] == relay[(frm["Dr"], by["Dc"])] and not sender else hi))
+        q.wait_ge(S["l%d" % frm["Dc"]], len(hi))
+        q.wait_ge(S["lar1"], 5 * len(off))
+        for h in (0, 64):
+            ev(q.dma_start(t[h:h + 64, :], T.lst[:, o:o + 64, :]), name, 16)
 
     kf, kc = T.kf, T.kc
     w(V, "io1")
-    ev(ts(T.kb[:, 0:1], T.ki[:, :], 15, None, A.bitwise_and), "c1")
-    ev(ts(T.kb[:, 1:2], T.ki[:, :], 4, None, A.arith_shift_right), "c1")
-    ev(ts(T.kb[:, 2:3], T.ki[:, :], 31, None, A.bitwise_and), "c1")
-    ev(ts(T.kb[:, 3:4], T.ki[:, :], 5, None, A.arith_shift_right), "c1")
-    ev(ts(T.x15[:, :], T.xi[:, 0:128], 15, None, A.bitwise_and), "c1")
+    for i, (op, s) in enumerate(((A.bitwise_and, 15), (A.arith_shift_right, 4), (A.bitwise_and, 63), (A.arith_shift_right, 6),
+                                 (A.bitwise_and, 7))):
+        ev(ts(T.kb[:, i:i + 1], T.ki[:, :], s, None, op), "c1")
+    ev(ts(T.xs6[:, :], T.xi[:, 0:128], 6, None, A.arith_shift_right), "c1")
+    ev(ts(T.xs3[:, :], T.xi[:, 0:16], 3, None, A.arith_shift_right), "c1")
     w(V, "c1")
-    ev(V.tensor_copy(out=kf[:, 0:4], in_=T.kb[:, :]), "c2")
-    ev(V.tensor_copy(out=kf[:, 4:5], in_=T.ki[:, :]), "c2")
+    ev(V.tensor_copy(out=kf[:, 0:5], in_=T.kb[:, 0:5]), "c2")
+    ev(V.tensor_copy(out=kf[:, 5:6], in_=T.ki[:, :]), "c2")
     w(V, "c2")
-    ev(ts(T.rep[0:16, :], T.x15[0:16, :], kf[0:16, 4:5], None, A.is_equal), "c3")
-    ev(ts(T.eye[:, :], T.xi[:, 0:128], kf[:, 4:5], None, A.is_equal), "c3")
-
-    if sender:
-        w(V, "lds")
-        w(V, "ldd")
-        src, dst = T.ld[0:16, 0:64], T.ld[0:16, 64:128]
-        d = lambda k: T.dg[0:16, 64 * k:64 * k + 64]
-        ev(ts(d(0), src, 0xF000, None, A.bitwise_and), "lo")
-        ev(ts(d(1), dst, 3, 0x1E00, A.arith_shift_right, A.bitwise_and), "lo")
-        ev(ts(d(2), src, 4032, None, A.bitwise_and), "lo")
-        ev(ts(d(3), src, 63, None, A.bitwise_and), "lo")
-        ev(ts(d(4), dst, 4064, None, A.bitwise_and), "lo")
-        ev(ts(d(5), dst, 31, None, A.bitwise_and), "lo")
-        w(V, "lo")
-        ev(V.tensor_tensor(out=T.xb[0:16, 0:64], in0=d(0), in1=d(1), op=A.add), "lx")
-        ev(V.tensor_copy(out=T.xb[0:16, 64:192], in_=T.dg[0:16, 128:256]), "lx")
-        ev(ts(T.xb[0:16, 192:256], d(4), float(PAD), None, A.add), "lx")
-        ev(V.tensor_copy(out=T.xb[0:16, 256:320], in_=d(5)), "lx")
-        w(P, "c3")
-        w(P, "lx")
-        ev(P.matmul(T.psl[:, 0:64], T.rep[0:16, :], T.xb[0:16, 0:64], True, True), "lp")
-        ev(P.matmul(T.psl[:, 64:80], T.xb[0:16, 64:320:2], T.eye[0:16, 0:16], True, True), "lp")
-        ev(P.matmul(T.psl[:, 80:96], T.xb[0:16, 65:320:2], T.eye[0:16, 0:16], True, True), "lp")
-        w(V, "lp")
-        ev(V.tensor_copy(out=T.lists[:, a, :], in_=T.psl[:, 0:96]), "lready")
-
-        w(g, "lready")
-        dests = [first[by[k]] for k in ("Fe", "Fo", "O1", "O2", "O0", "Dc", "Dr")]
-        dests += [c for c in (helper[by["Dc"]], helper[by["Dr"]], helper[a]) if c not in dests]
-        ids = []
-        for c in dests:
-            rid, pid = topo.addr(c, core)
-            ids.append(DstId(rid=rid, pnc=pid))
-        g.remote_dma_fused([RemoteDMATransfer(dst_ids=ids, dma_engine_mask=off_mask, remote_sem=S["l%d" % a],
-                                              srcs=[T.lists[:, a, :]], dsts=[T.lists[:, a, :]] * len(ids))], local_sem=S["lsent"])
-        Y.wait_ge(S["lsent"], len(eng))
-        ev(Y.dma_start(T.big[:, 0:R], T.tab[:, :]), "tabl", 16)
-
-    w(V, "c3")
-    w(V, "io2")
-    if sender:
-        ev(ts(kc[:, 0:1], kf[:, 1:2], 512.0, 4096.0 * a, A.mult, A.add), "k1")
-    else:
-        ev(ts(kc[:, 0:1], kf[:, 1:2], 4096.0, 512.0 * a, A.mult, A.add), "k1")
-    ev(ts(kc[:, 1:2], kf[:, 1:2], 256.0, float(SLOT0 - 1), A.mult, A.add), "k1")
-    ev(ts(kc[:, 2:3], kf[:, 2:3], 4.0, None, A.mult), "k1")
-    ev(ts(T.xs4[:, :], T.xi[:, 0:128], 4, None, A.arith_shift_right), "k1")
-    ev(ts(T.xs3[:, :], T.xi[:, 0:16], 3, None, A.arith_shift_right), "k1")
-    ev(V.memset(T.za[:, :], 0.0), "k1")
-    ev(V.memset(T.zc[:, :], 0.0), "k1")
-    ev(ts(T.lb[:, :], T.xi[:, 0:128], kf[:, 4:5], None, A.is_gt), "k1")
+    for k in range(4):
+        if sender:
+            ev(ts(kc[:, k:k + 1], kf[:, 3:4], 4.0, float(8 * a + k), A.mult, A.add), "k1")
+        else:
+            ev(ts(kc[:, k:k + 1], kf[:, 3:4], 32.0, float(8 * k + a), A.mult, A.add), "k1")
+        ev(ts(kc[:, 4 + k:5 + k], kf[:, 3:4], 1024.0, float(SLOT0 - 1 + 256 * k), A.mult, A.add), "k1")
+    ev(ts(kc[:, 8:9], kf[:, 2:3], 2.0, None, A.mult), "k1")
+    ev(ts(kc[:, 9:10], kf[:, 4:5], -8.0, None, A.add), "k1")
+    ev(ts(T.lb[:, :], T.xi[:, 0:128], kf[:, 5:6], None, A.is_gt), "k1")
+    ev(ts(T.la[:, :], T.xs6[:, :], kf[:, 3:4], None, A.is_equal), "k1")
+    ev(V.memset(T.seg[:, :], 1.0), "k1")
     if not sender:
-        ev(ts(kc[:, 4:5], kf[:, 0:1], -2.0, None, A.add), "k1")
-        ev(ts(kc[:, 5:6], kf[:, 0:1], 1.0, None, A.is_equal), "k1")
-        ev(ts(kc[:, 6:7], kf[:, 0:1], 0.0, None, A.is_equal), "k1")
-        ev(ts(kc[:, 7:8], kf[:, 1:2], 256.0, float(R), A.mult, A.add), "k1")
+        ev(ts(kc[:, 12:13], kf[:, 3:4], float(-PAD), float(PAD), A.mult, A.add), "k1")
+        ev(ts(kc[:, 13:14], kf[:, 0:1], 1.0, None, A.is_equal), "k1")
+        ev(ts(kc[:, 14:15], kf[:, 0:1], 0.0, None, A.is_equal), "k1")
+        ev(ts(kc[:, 15:16], kf[:, 1:2], 256.0, float(R), A.mult, A.add), "k1")
         ev(V.memset(T.xz[:, :], 0.0), "k1")
     w(V, "k1")
-    ev(V.tensor_tensor(out=kc[:, 3:4], in0=kc[:, 2:3], in1=kf[:, 3:4], op=A.add), "k2")
-    ev(ts(T.la[:, :], T.xs4[:, :], kf[:, 1:2], None, A.is_equal), "k2")
+    ev(V.tensor_tensor(out=kc[:, 10:11], in0=kc[:, 8:9], in1=kc[:, 9:10], op=A.subtract), "k2")
+    ev(V.tensor_tensor(out=kc[:, 11:12], in0=kc[:, 8:9], in1=kf[:, 3:4], op=A.add), "k2")
     if not sender:
-        ev(V.tensor_tensor(out=kc[:, 8:9], in0=kc[:, 6:7], in1=kc[:, 7:8], op=A.mult), "k2")
+        ev(V.tensor_tensor(out=kc[:, 16:17], in0=kc[:, 14:15], in1=kc[:, 15:16], op=A.mult), "k2")
     w(V, "k2")
+    ev(ts(T.um[:, :], T.xi[:, 0:144], kc[:, 10:11], None, A.is_equal), "k3")
+    for k in range(4):
+        ev(ts(T.zc[:, k, :], T.xi[:, 0:144], kc[:, 10:11], kc[:, 4 + k:5 + k], A.is_equal, A.mult), "k3")
     ev(V.tensor_tensor(out=T.ltri[:, :], in0=T.la[:, :], in1=T.lb[:, :], op=A.mult), "k3")
-    ev(ts(T.gx[:, :], T.xi[:, 0:144], kc[:, 3:4], None, A.is_equal), "k3")
+    ev(ts(T.gx[:, :], T.xi[:, 0:144], kc[:, 11:12], None, A.is_equal), "k3")
+    ev(V.memset(T.seg[:, SEG:SEG + 1], 0.0), "k3")
     ev(ts(T.wr[:, :], T.xs3[:, :], kf[:, 0:1], None, A.is_equal), "k3")
-    ev(ts(T.za[:, 112:128], T.xi[:, 0:16], kf[:, 0:1], None, A.is_equal), "k3")
-    ev(ts(T.zc[:, 112:128], T.xi[:, 0:16], kf[:, 0:1], kc[:, 1:2], A.is_equal, A.mult), "k3")
+    ev(ts(T.eye[:, :], T.xi[:, 0:128], kf[:, 5:6], None, A.is_equal), "k3")
     ev(V.memset(T.win[:, SLOT0:WIN], 0.0), "k3")
     if not sender:
-        ev(ts(T.wd[:, :], T.xi[:, 0:2], kc[:, 4:5], None, A.is_equal), "k3")
-        ev(ts(T.jl[:, :], T.xi[:, :], kc[:, 5:6], kc[:, 8:9], A.mult, A.add), "k3")
+        ev(ts(T.wd[:, :], T.xi[:, 0:2], kf[:, 0:1], None, A.is_equal), "k3")
+        ev(ts(T.jl[:, :], T.xi[:, :], kc[:, 13:14], kc[:, 16:17], A.mult, A.add), "k3")
         ev(ts(T.cown[:, :], T.xi[:, :], 16.0, kf[:, 0:1], A.mult, A.add), "k3")
         ev(V.memset(T.jwin[:, PAD:PAD + R], 0.0), "k3")
     w(V, "k3")
+    w(V, "io2")
 
-    def mrow(r):
-        ev(ts(T.mm[:, r:512:8], T.lists[:, r, 0:64], kc[:, 0:1], None, A.is_equal), "mrow")
-
+    w(V, "lds")
+    ev(ts(T.sb[:, :], T.s2[:, :], 9, 0x78, A.arith_shift_right, A.bitwise_and), "sh")
+    w(V, "ldd")
+    ev(ts(T.db[:, :], T.d2[:, :], 12, None, A.arith_shift_right), "sh")
+    w(V, "sh")
+    ev(V.tensor_tensor(out=T.cls[:, :], in0=T.sb[:, :], in1=T.db[:, :], op=A.add), "cl")
+    w(V, "cl")
     w(P, "k3")
-    for k in (None, "Dr", "Dc"):
-        s = a if k is None else frm[k]
-        if k is None and sender:
-            w(P, "lready")
-        else:
-            V.wait_ge(S["l%d" % s], 8)
-            P.wait_ge(S["l%d" % s], 8)
-        mrow(s)
-    V.wait_ge(S["lar1"], 40)
-    P.wait_ge(S["lar1"], 40)
-    for k in ("Fe", "Fo", "O0", "O1", "O2"):
-        mrow(frm[k])
-    w(V, "mrow")
-    ev(V.tensor_tensor_scan(out=T.pss[:, :], data0=T.mm[:, :], data1=T.mm[:, :], initial=0.0, op0=A.add, op1=A.max), "scn")
-    for s in range(4):
-        for e in range(2):
-            j = 2 * s + e
-            ev(P.matmul(T.psn[:, 128 * j:128 * j + 128], T.gx[:, 4 * s:4 * s + 128], T.lists[:, :, 64 + 16 * e:80 + 16 * e], True, True), "lnp")
-    w(C, "mrow")
-    ev(C.activation(T.junk[:, :], T.mm[:, :], F.Copy, accum_out=T.tot[:, :]), "tt")
+    mk = lambda k: T.mm[:, SEG * k + 1:SEG * k + SEG]
+    for k in range(4):
+        ev(ts(mk(k), T.cls[:, :], kc[:, k:k + 1], None, A.is_equal), "m%d" % k)
+        w(P, "m%d" % k)
+        for f in range(2):
+            P.matmul(T.pso[:, 0:64], T.zc[:, k, 8 - 8 * f:136 - 8 * f], T.mm[:, SEG * k + 1 + f:SEG * k + SEG:2], k == 0 and f == 0, False)
+        if k < 3:
+            w(C, "m%d" % k)
+            ev(C.activation(T.junk[:, 128 * k:128 * k + 128], mk(k), F.Copy, accum_out=T.tot[:, k:k + 1]), "tt")
+    w(V, "m3")
+    ev(V.tensor_reduce(out=T.tot[:, 3:4], in_=mk(3), axis=X.X, op=A.add), "tr3")
+    t = T.s2 if sender else T.d2
+    ev(ts(T.dg[0:64, :], t[0:64, :], 4032 if sender else 4064, None, A.bitwise_and), "dl")
+    ev(ts(T.dg[64:128, :], t[64:128, :], 63 if sender else 31, None, A.bitwise_and), "dl")
+    w(V, "dl")
+    if sender:
+        ev(V.tensor_copy(out=T.dgb[:, :], in_=T.dg[:, :]), "db2")
+    else:
+        ev(ts(T.dgb[:, :], T.dg[:, :], kc[:, 12:13], None, A.add), "db2")
     w(P, "tt")
-    ev(P.matmul(T.psb[:, 0:1], T.ltri[:, :], T.tot[:, :], True, True), "bas")
-    w(C, "lnp")
-    ev(C.activation(T.lin[:, 0:512], T.psn[:, 0:512], F.Copy), "lnc")
-    ev(C.activation(T.lin[:, 512:1024], T.psn[:, 512:1024], F.Copy), "lnc")
-    w(P, "mrow")
-    for q in range(8):
-        P.matmul(T.pso[:, 0:64], T.zc[:, 112 - 16 * q:240 - 16 * q], T.mm[:, 64 * q:64 * q + 64], q == 0, False)
-    w(V, "scn")
-    ev(V.tensor_tensor(out=T.me[:, :], in0=T.pss[:, :], in1=T.mm[:, :], op=A.mult), "ee")
+    w(P, "tr3")
+    ev(P.matmul(T.psb[:, 0:4], T.ltri[:, :], T.tot[:, :], True, True), "bas")
+    w(P, "db2")
+    for e in range(2):
+        for q in range(8):
+            ev(P.matmul(T.psn[:, 512 * e + q:512 * e + 512:8], T.gx[:, 2 * q:2 * q + 128], T.dgb[:, 64 * e:64 * e + 64], True, True), "ln%d" % e)
+        w(C, "ln%d" % e)
+        ev(C.activation(T.lin[:, 512 * e:512 * e + 512], T.psn[:, 512 * e:512 * e + 512], F.Copy), "lnc")
     w(V, "bas")
-    ev(ts(T.mb[:, :], T.mm[:, :], T.psb[:, 0:1], None, A.mult), "em")
-    w(P, "ee")
-    for q in range(8):
-        P.matmul(T.pso[:, 0:64], T.za[:, 112 - 16 * q:240 - 16 * q], T.me[:, 64 * q:64 * q + 64], False, False)
-    w(P, "em")
-    for q in range(8):
-        i = P.matmul(T.pso[:, 0:64], T.za[:, 112 - 16 * q:240 - 16 * q], T.mb[:, 64 * q:64 * q + 64], False, q == 7)
+    ev(V.tensor_copy(out=T.mm[:, 0:4 * SEG:SEG], in_=T.psb[:, 0:4]), "inj")
+    w(V, "inj")
+    hs = lambda x: slice(2 * SEG * x, 2 * SEG * x + 2 * SEG)
+    pc = [T.psa, T.psc]
+    for x in range(2):
+        ev(V.tensor_tensor_scan(out=pc[x][:, 0:2 * SEG], data0=T.seg[:, :], data1=T.mm[:, hs(x)], initial=0.0, op0=A.mult, op1=A.add), "sc%d" % x)
+    for x in range(2):
+        w(V, "sc%d" % x)
+        ev(V.tensor_tensor(out=T.me[:, hs(x)], in0=pc[x][:, 0:2 * SEG], in1=T.mm[:, hs(x)], op=A.mult), "ee%d" % x)
+        w(P, "ee%d" % x)
+        for k in (2 * x, 2 * x + 1):
+            for f in range(2):
+                i = P.matmul(T.pso[:, 0:64], T.um[:, 8 - 8 * f:136 - 8 * f], T.me[:, SEG * k + 1 + f:SEG * k + SEG:2], False, k == 3 and f == 1)
     ev(i, "po")
     w(V, "po")
     ev(V.tensor_tensor(out=T.offf[:, :], in0=T.pso[:, 0:64], in1=T.tr[:, :], op=A.max), "mx")
@@ -357,7 +372,7 @@ def _program(g, core, a, sender, T, topo, kind, relay, helper):
         w(V, "gc")
         ev(V.tensor_copy(out=T.jwin[:, 0:PAD + R].indirect(T.dof[:, 0:16]), in_=T.jl[:, :]), "js")
         w(P, "js")
-        to = [T.pss, T.pso]
+        to = [T.psa, T.pso]
         for h in range(2):
             b0 = PAD + 2048 * h
             for i in range(16):
@@ -379,9 +394,9 @@ def _program(g, core, a, sender, T, topo, kind, relay, helper):
             ev(V.tensor_copy(out=T.jo[:, j], in_=T.jf[:, j]), "jr%d" % h)
             w(g, "jr%d" % h)
             rid, pid = topo.addr(T.cores[a], core)
-            g.remote_dma(T.jo[:, j], T.jo[:, j], S["ja%d" % h], S["jsent"], pid, rid, off_mask)
-        g.wait_ge(S["jsent"], 2 * len(eng))
-        g.wait_ge(S["fsent"], 2 * len(eng))
+            g.remote_dma(T.jo[:, j], T.jo[:, j], S["ja%d" % h], S["jsent"], pid, rid, _mask(off))
+        g.wait_ge(S["jsent"], 2 * len(off))
+        g.wait_ge(S["fsent"], 2 * len(off))
         return
 
     for i in range(16):
@@ -394,51 +409,50 @@ def _program(g, core, a, sender, T, topo, kind, relay, helper):
     w(V, "pg")
     ev(V.tensor_copy(out=T.g16[:, :], in_=T.psg[:, 0:128]), "gc")
 
-    pairs = [("Fe", "Fo"), ("O1", "O2"), ("O0", "Dc"), ("Dr", None)]
     for q in (V, C):
         w(q, "gc")
         w(q, "tabl")
     own = slice(R + CAP * a, R + CAP * a + CAP)
 
-    def gat(q, out, win, off, name):
+    def gat(q, out, win, offs, name):
         if q is V:
-            ev(V.tensor_copy(out=out, in_=win.indirect(off)), name)
+            ev(V.tensor_copy(out=out, in_=win.indirect(offs)), name)
         else:
-            ev(C.activation(out, win.indirect(off), F.Copy, bias=-0.0), name)
+            ev(C.activation(out, win.indirect(offs), F.Copy, bias=-0.0), name)
 
     def place(k):
         if k is None:
             return a, T.big[:, own]
         return by[k], T.msg[:, CAP * by[k]:CAP * by[k] + CAP]
 
-    nsent = 0
-    for n, pr in enumerate(pairs):
+    calls = [[("Fe", off), ("O1", on)], [("Fo", off), ("O2", on)], [("O0", off + on)], [("Dc", lo), ("Dr", hi)]]
+    for n, pr in enumerate([("Fe", "O1"), ("Fo", "O2"), ("O0", "Dc"), ("Dr", None)]):
         for q, k in zip((V, C), pr):
             b, out = place(k)
             gat(q, out, T.big[:, 0:R], T.g16[:, 16 * b:16 * b + 16], "gp%d" % n)
         w(g, "gp%d" % n)
         trs = []
-        ks = [k for k in pr if k is not None]
-        for x, k in enumerate(ks):
+        for k, e in calls[n]:
             b = by[k]
-            rid, pid = topo.addr(first[b], core)
-            trs.append(RemoteDMATransfer(dst_ids=[DstId(rid=rid, pnc=pid)], dma_engine_mask=half[x] if len(ks) == 2 else off_mask,
+            trs.append(RemoteDMATransfer(dst_ids=_ids([first[b]], core, topo), dma_engine_mask=_mask(e),
                                          remote_sem=S["dar" if relay[(a, b)] is None else "dr"],
                                          srcs=[place(k)[1]], dsts=[T.big[:, own]]))
         g.remote_dma_fused(trs, local_sem=S["dsent"])
-        nsent += len(eng)
-    g.wait_ge(S["dsent"], nsent)
+    g.wait_ge(S["dsent"], sum(len(e) for c in calls for k, e in c))
 
     for q in (V, C):
         w(q, "gp3")
-        q.wait_ge(S["dar"], 5 * 8 + 8 + 4)
-        q.wait_ge(S["ja0"], 8)
-    for n in range(4):
-        q = (V, C)[n % 2]
-        if n == 2:
-            V.wait_ge(S["ja1"], 8)
-            C.wait_ge(S["ja1"], 8)
-        gat(q, T.yb[:, 1024 * n:1024 * n + 1024], T.big[:, :], T.jo[:, 64 * n:64 * n + 64], "yg%d" % n)
+        q.wait_ge(S["dar"], 5 * len(off) + len(lo) + len(hi))
+        q.wait_ge(S["ja0"], len(off))
+    second = []
+    for n, (s, c0, m) in enumerate(YBLK):
+        q = (V, C)[s]
+        if c0 + m > R // 2 and s not in second:
+            second.append(s)
+            q.wait_ge(S["ja1"], len(off))
+        gat(q, T.yb[:, c0:c0 + m], T.big[:, :], T.jo[:, c0 // 16:(c0 + m) // 16], "yg%d" % n)
+    for n in sorted(range(len(YBLK)), key=lambda n: sum(m for s, c0, m in YBLK[:n + 1] if s == YBLK[n][0])):
+        c0, m = YBLK[n][1:]
         w(Y, "yg%d" % n)
-        ev(Y.dma_start(T.y[:, 1024 * n:1024 * n + 1024], T.yb[:, 1024 * n:1024 * n + 1024]), "ys", 16)
+        ev(Y.dma_start(T.y[:, c0:c0 + m], T.yb[:, c0:c0 + m]), "ys", 16)
     w(Y, "ys")

from concourse.bass import DstId, RemoteDMATransfer
from concourse.mybir import AluOpType as A, ActivationFunctionType as F, AxisListType as X

N, R, CAP = 8, 4096, 256
PAD = 384
SLOT0 = 1153
WIN = SLOT0 + N * CAP
SEG = 129

SCRATCH = {
    "lst": ("dram", [N, 128, 16], "int32"),
    "s2": ("sbuf", [128, 128], "int32"),
    "d2": ("sbuf", [128, 128], "int32"),
    "sb": ("sbuf", [128, 128], "int32"),
    "db": ("sbuf", [128, 128], "int32"),
    "dg": ("sbuf", [128, 128], "int32"),
    "dgb": ("sbuf", [128, 128], "bfloat16"),
    "cls": ("sbuf", [128, 128], "bfloat16"),
    "ki": ("sbuf", [128, 1], "int32"),
    "xi": ("sbuf", [128, 256], "int32"),
    "ti": ("sbuf", [128, 16], "float32"),
    "tr": ("sbuf", [128, 64], "float32"),
    "kb": ("sbuf", [128, 8], "int32"),
    "kf": ("sbuf", [128, 8], "float32"),
    "kc": ("sbuf", [128, 32], "float32"),
    "xs6": ("sbuf", [128, 128], "int32"),
    "xs3": ("sbuf", [128, 16], "int32"),
    "eye": ("sbuf", [128, 128], "bfloat16"),
    "um": ("sbuf", [128, 144], "bfloat16"),
    "zc": ("sbuf", [128, 4, 144], "bfloat16"),
    "la": ("sbuf", [128, 128], "float32"),
    "lb": ("sbuf", [128, 128], "float32"),
    "ltri": ("sbuf", [128, 128], "float32"),
    "gx": ("sbuf", [128, 144], "bfloat16"),
    "seg": ("sbuf", [128, 2 * SEG], "bfloat16"),
    "wr": ("sbuf", [128, 16], "bfloat16"),
    "wd": ("sbuf", [128, 2], "bfloat16"),
    "jl": ("sbuf", [128, 256], "bfloat16"),
    "cown": ("sbuf", [128, 256], "float32"),
    "mm": ("sbuf", [128, 4 * SEG], "bfloat16"),
    "me": ("sbuf", [128, 4 * SEG], "bfloat16"),
    "junk": ("sbuf", [128, 512], "bfloat16"),
    "tot": ("sbuf", [128, 4], "float32"),
    "lin": ("sbuf", [128, 1024], "bfloat16"),
    "offf": ("sbuf", [128, 64], "float32"),
    "offs": ("sbuf", [128, 64], "uint16"),
    "win": ("sbuf", [128, WIN + 7], "bfloat16"),
    "xsb": ("sbuf", [128, 512], "bfloat16"),
    "xz": ("sbuf", [128, 480], "bfloat16"),
    "g16": ("sbuf", [128, 128], "uint16"),
    "dsf": ("sbuf", [128, 16], "float32"),
    "dof": ("sbuf", [128, 16], "uint16"),
    "jwin": ("sbuf", [128, PAD + R], "bfloat16"),
    "jf": ("sbuf", [128, 256], "float32"),
    "jo": ("sbuf", [128, 256], "uint16"),
    "big": ("sbuf", [128, R + N * CAP], "bfloat16"),
    "msg": ("sbuf", [128, N * CAP], "bfloat16"),
    "yb": ("sbuf", [128, R], "bfloat16"),
    "psa": ("psum", [128, 512], "float32"),
    "psc": ("psum", [128, 512], "float32"),
    "psb": ("psum", [128, 512], "float32"),
    "pso": ("psum", [128, 512], "float32"),
    "psn": ("psum", [128, 1024], "float32"),
    "psx": ("psum", [128, 512], "float32"),
    "psg": ("psum", [128, 512], "float32"),
}
YBLK = [(0, 0, 512), (1, 512, 768), (1, 1280, 768), (0, 2048, 1024), (0, 3072, 512), (1, 3584, 512)]
_EV = ["io1", "io2", "c1", "c2", "c3", "own", "lds", "ldd", "k1", "k2", "k3", "tabl", "sh", "cl", "m0", "m1", "m2", "m3",
       "dl", "db2", "tt", "tr3", "bas", "inj", "sc0", "sc1", "ee0", "ee1", "po", "mx", "of", "ln0", "ln1", "lnc", "sc", "x1", "xc1",
       "pg", "gc", "dx", "dm", "js", "jx0", "jx1", "jc0", "jc1", "jp0", "jp1", "jm0", "jm1", "jr0", "jr1"]
SEMAPHORES = (_EV + ["gp%d" % k for k in range(4)] + ["l%d" % k for k in range(N)] + ["yg%d" % k for k in range(len(YBLK))]
              + ["lar1", "lsent", "dsent", "fsent", "dr", "dar", "ja0", "ja1", "jsent", "ys"])


def _chip_cores(core, topo):
    return [c for c in range(128 * topo.host(core), 128 * topo.host(core) + 128) if topo.chip(c) == topo.chip(core)]


def _bits(m):
    return [i for i in range(16) if (m >> i) & 1]


def _mask(bits):
    return sum(1 << e for e in bits)


def _routes(T, topo):
    cores = T.cores
    kind, relay, used = {}, {}, set(cores)
    helper = {}

    def take(near, dst, other_die):
        cand = [c for c in _chip_cores(near, topo) if c not in used and topo.may_write(c, dst)]
        cand.sort(key=lambda c: (sum(1 for d in cores if topo.may_write(c, d)), (topo.die(c) == topo.die(near)) == other_die, c))
        used.add(cand[0])
        return cand[0]

    n = len(cores)
    for a in range(n):
        for b in range(n):
            if a == b:
                continue
            ca, cb = cores[a], cores[b]
            if topo.may_write(ca, cb):
                kind[(a, b)] = "Dr" if topo.same_plane(ca, cb) else "Dc"
                relay[(a, b)] = None
    reach = lambda a, b: any(topo.may_write(c, cores[b]) for c in _chip_cores(cores[a], topo))
    for a in range(n):
        nb = {kind[(a, x)]: x for x in range(n) if (a, x) in kind and kind[(a, x)] in ("Dr", "Dc")}
        for b in range(n):
            if a != b and not reach(a, b):
                same = topo.chip(cores[a]) == topo.chip(cores[b])
                kind[(a, b)] = "Fe" if same else "Fo"
                relay[(a, b)] = take(cores[nb["Dr" if same else "Dc"]], cores[b], same)
                if same:
                    helper[nb["Dr"]] = relay[(a, b)]
    for a in range(n):
        for b in range(n):
            if a != b and (a, b) not in kind:
                ca, cb = cores[a], cores[b]
                if topo.host(ca) == topo.host(cb):
                    kind[(a, b)] = "O0"
                elif topo.rack(topo.host(ca)) == topo.rack(topo.host(cb)):
                    kind[(a, b)] = "O1"
                else:
                    kind[(a, b)] = "O2"
                relay[(a, b)] = take(ca, cb, True)
    return kind, relay, helper


def _engines(core, a, T, topo, kind, relay, helper):
    by = {kind[(a, b)]: b for b in range(N) if b != a}
    off = _bits(topo.mask(T.cores[a], T.cores[by["Dr"]]))
    on = [e for e in _bits(topo.mask(T.cores[a], helper[a])) if e not in off]
    return off, off[:len(off) // 2], off[len(off) // 2:], on


_CACHE = {}


def rank_program(g, core, T, topo):
    if "r" not in _CACHE:
        _CACHE["r"] = _routes(T, topo)
    kind, relay, helper = _CACHE["r"]
    rank = T.rank_of(core)
    if rank is not None:
        return _program(g, core, rank, True, T, topo, kind, relay, helper)
    for a, c in helper.items():
        if c == core:
            return _program(g, core, a, False, T, topo, kind, relay, helper)
    for (a, b), c in relay.items():
        if c == core:
            _list_on(g, core, a, b, T, topo, kind, relay, helper)
            _data_on(g, core, a, b, T, topo, kind, relay, helper)
            g.wait_ge(T.sem["fsent"], 2 * len(_bits(topo.mask(core, T.cores[b]))))


def _ids(dests, core, topo):
    out = []
    for c in dests:
        rid, pid = topo.addr(c, core)
        out.append(DstId(rid=rid, pnc=pid))
    return out


def _list_on(g, core, a, b, T, topo, kind, relay, helper):
    S = T.sem
    off, lo, hi, on = _engines(core, a, T, topo, kind, relay, helper)
    dst = [T.cores[b], helper[b]]
    g.wait_ge(S["l%d" % a], len(lo))
    g.remote_dma_fused([RemoteDMATransfer(dst_ids=_ids(dst, core, topo), dma_engine_mask=topo.mask(core, dst[0]), remote_sem=S["lar1"],
                                          srcs=[T.lst[a]], dsts=[T.lst[a]] * 2)], local_sem=S["fsent"])


def _data_on(g, core, a, b, T, topo, kind, relay, helper):
    S = T.sem
    off, lo, hi, on = _engines(core, a, T, topo, kind, relay, helper)
    rid, pid = topo.addr(T.cores[b], core)
    slot = T.big[:, R + CAP * a:R + CAP * a + CAP]
    g.wait_ge(S["dr"], len(off) + len(on) if kind[(a, b)] == "O0" else len(on) if kind[(a, b)] in ("O1", "O2") else len(off))
    g.remote_dma(slot, slot, S["dar"], S["fsent"], pid, rid, topo.mask(core, T.cores[b]))


def _program(g, core, a, sender, T, topo, kind, relay, helper):
    S = T.sem
    V, P, C, Y = g.vector, g.tensor, g.scalar, g.sync
    cnt = {}

    def ev(ins, name, n=1):
        ins.then_inc(S[name], n)
        cnt[name] = cnt.get(name, 0) + n

    def w(q, name):
        q.wait_ge(S[name], cnt[name])

    def ts(out, in0, s1, s2, op0, op1=None):
        if op1 is None:
            return V.tensor_scalar(out=out, in0=in0, scalar1=s1, scalar2=None, op0=op0)
        return V.tensor_scalar(out=out, in0=in0, scalar1=s1, scalar2=s2, op0=op0, op1=op1)

    by = {kind[(a, b)]: b for b in range(N) if b != a}
    frm = {kind[(s, a)]: s for s in range(N) if s != a}
    first = {b: (T.cores[b] if relay[(a, b)] is None else relay[(a, b)]) for b in range(N) if b != a}
    off, lo, hi, on = _engines(core, a, T, topo, kind, relay, helper)

    XW = 144 if sender else 256
    if sender:
        ev(Y.dma_start(T.lst[a, 0:64, :], T.src[:, :]), "own", 16)
        ev(C.dma_start(T.lst[a, 64:128, :], T.dst[:, :]), "own", 16)
    ev(g.iota(T.ki[:, :], [[1, 1]], 0, 1), "io1")
    ev(g.iota(T.xi[:, 0:XW], [[1, XW]], 0, 0), "io1")
    if sender:
        w(g, "own")
        near = [first[by[k]] for k in ("Fe", "Fo", "O1", "O2", "O0")]
        far = [first[by[k]] for k in ("Dc", "Dr")]
        far += [c for c in (helper[by["Dc"]], helper[by["Dr"]]) if c not in near]

        def send(parts):
            g.remote_dma_fused([RemoteDMATransfer(dst_ids=_ids(d, core, topo), dma_engine_mask=_mask(e), remote_sem=S["l%d" % a],
                                                  srcs=[T.lst[a]], dsts=[T.lst[a]] * len(d)) for d, e in parts], local_sem=S["lsent"])
        send([(near, lo)])
        send([(far, hi), ([helper[a]], on)])
    ev(g.iota(T.tr[:, :], [[16, 64]], 0, 1, allow_small_or_imprecise_dtypes=True), "io2")
    if not sender:
        ev(g.iota(T.ti[:, :], [[16, 16]], 0, 1, allow_small_or_imprecise_dtypes=True), "io2")
        served = [ab for ab in relay if relay[ab] == core][0]
        _list_on(g, core, served[0], served[1], T, topo, kind, relay, helper)
        _data_on(g, core, served[0], served[1], T, topo, kind, relay, helper)
    else:
        Y.wait_ge(S["lsent"], len(lo) + len(hi) + len(on))
        ev(Y.dma_start(T.big[:, 0:R], T.tab[:, :]), "tabl", 16)

    for q, t, o, name in ((Y, T.s2, 0, "lds"), (C, T.d2, 64, "ldd")):
        if sender:
            w(q, "own")
        else:
            q.wait_ge(S["l%d" % a], len(on))
        q.wait_ge(S["l%d" % frm["Dr"]], len(lo if helper[a] == relay[(frm["Dr"], by["Dc"])] and not sender else hi))
        q.wait_ge(S["l%d" % frm["Dc"]], len(hi))
        q.wait_ge(S["lar1"], 5 * len(off))
        for h in (0, 64):
            ev(q.dma_start(t[h:h + 64, :], T.lst[:, o:o + 64, :]), name, 16)

    kf, kc = T.kf, T.kc
    w(V, "io1")
    for i, (op, s) in enumerate(((A.bitwise_and, 15), (A.arith_shift_right, 4), (A.bitwise_and, 63), (A.arith_shift_right, 6),
                                 (A.bitwise_and, 7))):
        ev(ts(T.kb[:, i:i + 1], T.ki[:, :], s, None, op), "c1")
    ev(ts(T.xs6[:, :], T.xi[:, 0:128], 6, None, A.arith_shift_right), "c1")
    ev(ts(T.xs3[:, :], T.xi[:, 0:16], 3, None, A.arith_shift_right), "c1")
    w(V, "c1")
    ev(V.tensor_copy(out=kf[:, 0:5], in_=T.kb[:, 0:5]), "c2")
    ev(V.tensor_copy(out=kf[:, 5:6], in_=T.ki[:, :]), "c2")
    w(V, "c2")
    for k in range(4):
        if sender:
            ev(ts(kc[:, k:k + 1], kf[:, 3:4], 4.0, float(8 * a + k), A.mult, A.add), "k1")
        else:
            ev(ts(kc[:, k:k + 1], kf[:, 3:4], 32.0, float(8 * k + a), A.mult, A.add), "k1")
        ev(ts(kc[:, 4 + k:5 + k], kf[:, 3:4], 1024.0, float(SLOT0 - 1 + 256 * k), A.mult, A.add), "k1")
    ev(ts(kc[:, 8:9], kf[:, 2:3], 2.0, None, A.mult), "k1")
    ev(ts(kc[:, 9:10], kf[:, 4:5], -8.0, None, A.add), "k1")
    ev(ts(T.lb[:, :], T.xi[:, 0:128], kf[:, 5:6], None, A.is_gt), "k1")
    ev(ts(T.la[:, :], T.xs6[:, :], kf[:, 3:4], None, A.is_equal), "k1")
    ev(V.memset(T.seg[:, :], 1.0), "k1")
    if not sender:
        ev(ts(kc[:, 12:13], kf[:, 3:4], float(-PAD), float(PAD), A.mult, A.add), "k1")
        ev(ts(kc[:, 13:14], kf[:, 0:1], 1.0, None, A.is_equal), "k1")
        ev(ts(kc[:, 14:15], kf[:, 0:1], 0.0, None, A.is_equal), "k1")
        ev(ts(kc[:, 15:16], kf[:, 1:2], 256.0, float(R), A.mult, A.add), "k1")
        ev(V.memset(T.xz[:, :], 0.0), "k1")
    w(V, "k1")
    ev(V.tensor_tensor(out=kc[:, 10:11], in0=kc[:, 8:9], in1=kc[:, 9:10], op=A.subtract), "k2")
    ev(V.tensor_tensor(out=kc[:, 11:12], in0=kc[:, 8:9], in1=kf[:, 3:4], op=A.add), "k2")
    if not sender:
        ev(V.tensor_tensor(out=kc[:, 16:17], in0=kc[:, 14:15], in1=kc[:, 15:16], op=A.mult), "k2")
    w(V, "k2")
    ev(ts(T.um[:, :], T.xi[:, 0:144], kc[:, 10:11], None, A.is_equal), "k3")
    for k in range(4):
        ev(ts(T.zc[:, k, :], T.xi[:, 0:144], kc[:, 10:11], kc[:, 4 + k:5 + k], A.is_equal, A.mult), "k3")
    ev(V.tensor_tensor(out=T.ltri[:, :], in0=T.la[:, :], in1=T.lb[:, :], op=A.mult), "k3")
    ev(ts(T.gx[:, :], T.xi[:, 0:144], kc[:, 11:12], None, A.is_equal), "k3")
    ev(V.memset(T.seg[:, SEG:SEG + 1], 0.0), "k3")
    ev(ts(T.wr[:, :], T.xs3[:, :], kf[:, 0:1], None, A.is_equal), "k3")
    ev(ts(T.eye[:, :], T.xi[:, 0:128], kf[:, 5:6], None, A.is_equal), "k3")
    ev(V.memset(T.win[:, SLOT0:WIN], 0.0), "k3")
    if not sender:
        ev(ts(T.wd[:, :], T.xi[:, 0:2], kf[:, 0:1], None, A.is_equal), "k3")
        ev(ts(T.jl[:, :], T.xi[:, :], kc[:, 13:14], kc[:, 16:17], A.mult, A.add), "k3")
        ev(ts(T.cown[:, :], T.xi[:, :], 16.0, kf[:, 0:1], A.mult, A.add), "k3")
        ev(V.memset(T.jwin[:, PAD:PAD + R], 0.0), "k3")
    w(V, "k3")
    w(V, "io2")

    w(V, "lds")
    ev(ts(T.sb[:, :], T.s2[:, :], 9, 0x78, A.arith_shift_right, A.bitwise_and), "sh")
    w(V, "ldd")
    ev(ts(T.db[:, :], T.d2[:, :], 12, None, A.arith_shift_right), "sh")
    w(V, "sh")
    ev(V.tensor_tensor(out=T.cls[:, :], in0=T.sb[:, :], in1=T.db[:, :], op=A.add), "cl")
    w(V, "cl")
    w(P, "k3")
    mk = lambda k: T.mm[:, SEG * k + 1:SEG * k + SEG]
    for k in range(4):
        ev(ts(mk(k), T.cls[:, :], kc[:, k:k + 1], None, A.is_equal), "m%d" % k)
        w(P, "m%d" % k)
        for f in range(2):
            P.matmul(T.pso[:, 0:64], T.zc[:, k, 8 - 8 * f:136 - 8 * f], T.mm[:, SEG * k + 1 + f:SEG * k + SEG:2], k == 0 and f == 0, False)
        if k < 3:
            w(C, "m%d" % k)
            ev(C.activation(T.junk[:, 128 * k:128 * k + 128], mk(k), F.Copy, accum_out=T.tot[:, k:k + 1]), "tt")
    w(V, "m3")
    ev(V.tensor_reduce(out=T.tot[:, 3:4], in_=mk(3), axis=X.X, op=A.add), "tr3")
    t = T.s2 if sender else T.d2
    ev(ts(T.dg[0:64, :], t[0:64, :], 4032 if sender else 4064, None, A.bitwise_and), "dl")
    ev(ts(T.dg[64:128, :], t[64:128, :], 63 if sender else 31, None, A.bitwise_and), "dl")
    w(V, "dl")
    if sender:
        ev(V.tensor_copy(out=T.dgb[:, :], in_=T.dg[:, :]), "db2")
    else:
        ev(ts(T.dgb[:, :], T.dg[:, :], kc[:, 12:13], None, A.add), "db2")
    w(P, "tt")
    w(P, "tr3")
    ev(P.matmul(T.psb[:, 0:4], T.ltri[:, :], T.tot[:, :], True, True), "bas")
    w(P, "db2")
    for e in range(2):
        for q in range(8):
            ev(P.matmul(T.psn[:, 512 * e + q:512 * e + 512:8], T.gx[:, 2 * q:2 * q + 128], T.dgb[:, 64 * e:64 * e + 64], True, True), "ln%d" % e)
        w(C, "ln%d" % e)
        ev(C.activation(T.lin[:, 512 * e:512 * e + 512], T.psn[:, 512 * e:512 * e + 512], F.Copy), "lnc")
    w(V, "bas")
    ev(V.tensor_copy(out=T.mm[:, 0:4 * SEG:SEG], in_=T.psb[:, 0:4]), "inj")
    w(V, "inj")
    hs = lambda x: slice(2 * SEG * x, 2 * SEG * x + 2 * SEG)
    pc = [T.psa, T.psc]
    for x in range(2):
        ev(V.tensor_tensor_scan(out=pc[x][:, 0:2 * SEG], data0=T.seg[:, :], data1=T.mm[:, hs(x)], initial=0.0, op0=A.mult, op1=A.add), "sc%d" % x)
    for x in range(2):
        w(V, "sc%d" % x)
        ev(V.tensor_tensor(out=T.me[:, hs(x)], in0=pc[x][:, 0:2 * SEG], in1=T.mm[:, hs(x)], op=A.mult), "ee%d" % x)
        w(P, "ee%d" % x)
        for k in (2 * x, 2 * x + 1):
            for f in range(2):
                i = P.matmul(T.pso[:, 0:64], T.um[:, 8 - 8 * f:136 - 8 * f], T.me[:, SEG * k + 1 + f:SEG * k + SEG:2], False, k == 3 and f == 1)
    ev(i, "po")
    w(V, "po")
    ev(V.tensor_tensor(out=T.offf[:, :], in0=T.pso[:, 0:64], in1=T.tr[:, :], op=A.max), "mx")
    w(V, "mx")
    ev(V.tensor_copy(out=T.offs[:, :], in_=T.offf[:, :]), "of")
    w(V, "of")
    w(V, "lnc")
    ev(V.tensor_copy(out=T.win[:, 0:WIN].indirect(T.offs[:, 0:64]), in_=T.lin[:, :]), "sc")
    w(P, "sc")
    wslot = lambda i: T.win[:, SLOT0 + i:SLOT0 + i + 2033:16]

    if not sender:
        for i in range(16):
            ev(P.matmul(T.psx[:, i:32:16], wslot(i), T.wd[:, :], True, True), "x1")
        w(V, "x1")
        ev(V.tensor_copy(out=T.xz[:, 112:128], in_=T.psx[:, 0:16]), "dx")
        ev(V.tensor_copy(out=T.xz[:, 352:368], in_=T.psx[:, 16:32]), "dx")
        w(P, "dx")
        for s in range(N):
            for d in (0, 240):
                i = P.matmul(T.psg[:, 0:16], T.xz[:, d + 112 - 16 * s:d + 240 - 16 * s], T.eye[:, 16 * s:16 * s + 16],
                             s == 0 and d == 0, s == N - 1 and d == 240)
        ev(i, "pg")
        w(V, "pg")
        ev(V.tensor_tensor(out=T.dsf[:, :], in0=T.psg[:, 0:16], in1=T.ti[:, :], op=A.max), "dm")
        w(V, "dm")
        ev(V.tensor_copy(out=T.dof[:, :], in_=T.dsf[:, :]), "gc")
        w(V, "gc")
        ev(V.tensor_copy(out=T.jwin[:, 0:PAD + R].indirect(T.dof[:, 0:16]), in_=T.jl[:, :]), "js")
        w(P, "js")
        to = [T.psa, T.pso]
        for h in range(2):
            b0 = PAD + 2048 * h
            for i in range(16):
                ev(P.matmul(T.psn[:, 512 * h + i:512 * h + 256:16], T.jwin[:, b0 + i:b0 + i + 2033:16], T.wr[:, :], True, True), "jx%d" % h)
            x0 = 256 * h
            if h == 0:
                w(V, "jx0")
                ev(V.tensor_copy(out=T.xsb[:, 0:256], in_=T.psn[:, 0:256]), "jc0")
            else:
                w(C, "jx1")
                ev(C.activation(T.xsb[:, 256:512], T.psn[:, 512:768], F.Copy), "jc1")
            w(P, "jc%d" % h)
            P.matmul(to[h][:, 0:128], T.xsb[:, x0:x0 + 128], T.eye[:, :], True, False)
            ev(P.matmul(to[h][:, 0:128], T.xsb[:, x0 + 128:x0 + 256], T.eye[:, :], False, True), "jp%d" % h)
            j = slice(128 * h, 128 * h + 128)
            w(V, "jp%d" % h)
            ev(V.tensor_tensor(out=T.jf[:, j], in0=to[h][:, 0:128], in1=T.cown[:, j], op=A.max), "jm%d" % h)
            w(V, "jm%d" % h)
            ev(V.tensor_copy(out=T.jo[:, j], in_=T.jf[:, j]), "jr%d" % h)
            w(g, "jr%d" % h)
            rid, pid = topo.addr(T.cores[a], core)
            g.remote_dma(T.jo[:, j], T.jo[:, j], S["ja%d" % h], S["jsent"], pid, rid, _mask(off))
        g.wait_ge(S["jsent"], 2 * len(off))
        g.wait_ge(S["fsent"], 2 * len(off))
        return

    for i in range(16):
        ev(P.matmul(T.psx[:, i:256:16], wslot(i), T.wr[:, :], True, True), "x1")
    w(V, "x1")
    ev(V.tensor_copy(out=T.xsb[:, 0:256], in_=T.psx[:, 0:256]), "xc1")
    w(P, "xc1")
    P.matmul(T.psg[:, 0:128], T.xsb[:, 0:128], T.eye[:, :], True, False)
    ev(P.matmul(T.psg[:, 0:128], T.xsb[:, 128:256], T.eye[:, :], False, True), "pg")
    w(V, "pg")
    ev(V.tensor_copy(out=T.g16[:, :], in_=T.psg[:, 0:128]), "gc")

    for q in (V, C):
        w(q, "gc")
        w(q, "tabl")
    own = slice(R + CAP * a, R + CAP * a + CAP)

    def gat(q, out, win, offs, name):
        if q is V:
            ev(V.tensor_copy(out=out, in_=win.indirect(offs)), name)
        else:
            ev(C.activation(out, win.indirect(offs), F.Copy, bias=-0.0), name)

    def place(k):
        if k is None:
            return a, T.big[:, own]
        return by[k], T.msg[:, CAP * by[k]:CAP * by[k] + CAP]

    calls = [[("Fe", off), ("O1", on)], [("Fo", off), ("O2", on)], [("O0", off + on)], [("Dc", lo), ("Dr", hi)]]
    for n, pr in enumerate([("Fe", "O1"), ("Fo", "O2"), ("O0", "Dc"), ("Dr", None)]):
        for q, k in zip((V, C), pr):
            b, out = place(k)
            gat(q, out, T.big[:, 0:R], T.g16[:, 16 * b:16 * b + 16], "gp%d" % n)
        w(g, "gp%d" % n)
        trs = []
        for k, e in calls[n]:
            b = by[k]
            trs.append(RemoteDMATransfer(dst_ids=_ids([first[b]], core, topo), dma_engine_mask=_mask(e),
                                         remote_sem=S["dar" if relay[(a, b)] is None else "dr"],
                                         srcs=[place(k)[1]], dsts=[T.big[:, own]]))
        g.remote_dma_fused(trs, local_sem=S["dsent"])
    g.wait_ge(S["dsent"], sum(len(e) for c in calls for k, e in c))

    for q in (V, C):
        w(q, "gp3")
        q.wait_ge(S["dar"], 5 * len(off) + len(lo) + len(hi))
        q.wait_ge(S["ja0"], len(off))
    second = []
    for n, (s, c0, m) in enumerate(YBLK):
        q = (V, C)[s]
        if c0 + m > R // 2 and s not in second:
            second.append(s)
            q.wait_ge(S["ja1"], len(off))
        gat(q, T.yb[:, c0:c0 + m], T.big[:, :], T.jo[:, c0 // 16:(c0 + m) // 16], "yg%d" % n)
    for n in sorted(range(len(YBLK)), key=lambda n: sum(m for s, c0, m in YBLK[:n + 1] if s == YBLK[n][0])):
        c0, m = YBLK[n][1:]
        w(Y, "yg%d" % n)
        ev(Y.dma_start(T.y[:, c0:c0 + m], T.yb[:, c0:c0 + m]), "ys", 16)
    w(Y, "ys")
